import numpy as np
import ml_dtypes


def mxq(x, axis, fmt="e4m3"):
    dtype, down = {"e4m3": (ml_dtypes.float8_e4m3fn, 7), "e5m2": (ml_dtypes.float8_e5m2, 14)}[fmt]
    v = np.moveaxis(np.asarray(x, np.float32).astype(ml_dtypes.bfloat16).astype(np.float64), axis, -1)
    blocks = v.reshape(v.shape[:-1] + (-1, 32))
    amax = np.abs(blocks).max(-1, keepdims=True)
    byte = np.maximum(np.where(amax > 0, np.frexp(amax)[1] - 1 + 127, 0) - down, 1)
    scale = np.exp2(byte - 127.0)
    codes = (blocks / scale).astype(np.float32).astype(dtype).astype(np.float64)
    return np.moveaxis((codes * scale).reshape(v.shape), -1, axis)


WIDE = False


def mx_kscale(k):
    if not WIDE:
        return np.ones(k)
    levels = np.array([10, -10, 5, -5, 0])
    if k % 512:
        return np.exp2(np.random.permutation(np.resize(levels, k // 32))).repeat(32)
    a = np.empty((k // 512, 16))
    for p in range(k // 512):
        a[p, :8] = np.random.permutation(np.resize(levels, 8))
        for g in range(8):
            far = levels[np.abs(levels - a[p, g]) >= 10]
            a[p, g + 8] = far[np.random.randint(len(far))]
    return np.exp2(a.ravel()).repeat(32)


def f64(x):
    return np.asarray(x).astype(np.float64)


def striped(idx):
    return np.tile(idx.reshape(-1, 16).T, (8, 1)).astype(np.uint16)


def unstriped(offs):
    return offs[:16].T.reshape(-1).astype(np.int64)


def striped8(idx):
    return np.concatenate([x.reshape(-1, 16).T for x in idx]).astype(np.uint16)


def runs(offs, k):
    lists = np.stack([offs[16 * r : 16 * r + 16].T.reshape(-1) for r in range(8)]).astype(np.int64)
    return lists[np.arange(k) % 512 // 64]


def pack_weight(w):
    k, n = w.shape
    w = f64(np.asarray(w, np.float32).astype(ml_dtypes.bfloat16)).reshape(k // 32, 32, n)
    amax = np.abs(w).max(1)
    byte = np.clip(np.where(amax > 0, np.frexp(amax)[1] - 1 + 127 - 7, 1), 1, 254)
    scaled = (w * np.exp2(127.0 - byte)[:, None, :]).reshape(k, n).astype(np.float32)
    words = np.ascontiguousarray(scaled.reshape(k // 512, 128, 4, n).transpose(0, 1, 3, 2)).astype(ml_dtypes.float8_e4m3fn).view(np.uint8)
    return words, np.ascontiguousarray(byte.astype(np.uint8).reshape(k // 512, 16, n))


def unpack_weight(words, scales):
    g, p, n, _ = words.shape
    vals = np.ascontiguousarray(words).view(ml_dtypes.float8_e4m3fn).astype(np.float64) * np.repeat(np.exp2(scales.astype(np.float64) - 127.0), 8, axis=1)[..., None]
    return vals.transpose(0, 1, 3, 2).reshape(g * 512, n)


K, T, S, N, H = 512, 2048, 512, 512, 512


def setup_inputs():
    n = np.random.standard_normal
    s = mx_kscale(K)[:, None]
    u = mx_kscale(H)
    packed_xT = pack_weight(n((K, T)) * s)
    return {
        "x_words": packed_xT[0],
        "x_scales": packed_xT[1],
        "w1": (n((K, H)) / np.sqrt(K) / s).astype(np.float32),
        "gn": (np.random.uniform(0.5, 1.5, (H, 1)) * u[:, None]).astype(np.float32),
        "gm": (np.random.uniform(0.5, 1.5, (H, 1)) * u[:, None]).astype(np.float32),
        "w2": (n((H, N)) / np.sqrt(2 * H) / u[:, None]).astype(np.float32),
        "w3": (n((H, N)) / np.sqrt(2 * H) / u[:, None]).astype(np.float32),
        "offs": striped(np.random.permutation(T)[:S]),
        "n1": striped8(np.stack([np.random.permutation(S) for _ in range(8)])),
        "n2": striped8(np.stack([np.random.permutation(S) for _ in range(8)])),
        "n3": striped8(np.stack([np.random.permutation(S) for _ in range(8)])),
        "n4": striped8(np.stack([np.random.permutation(S) for _ in range(8)])),
        "n5": striped8(np.stack([np.random.permutation(S) for _ in range(8)])),
        "n6": striped8(np.stack([np.random.permutation(S) for _ in range(8)])),
    }


def reference(x_words, x_scales, w1, gn, gm, w2, w3, offs, n1, n2, n3, n4, n5, n6):
    xq = unpack_weight(x_words, x_scales)[:, unstriped(offs)]
    y = mxq(f64(w1), 0, "e4m3").T @ xq
    pa = y[np.arange(H)[:, None], runs(n1, H)]
    z = f64(gn) * ((2.0 * (y * pa)) / ((y) ** 2 + (pa) ** 2 + 0.5))
    pa2 = y[np.arange(H)[:, None], runs(n2, H)]
    pb = y[np.arange(H)[:, None], runs(n3, H)]
    z2 = f64(gm) * (np.maximum(np.maximum(y, pa2), pb) - (0.5 * (np.minimum(np.minimum(y, pa2), pb))))
    h = mxq(f64(w2), 0, "e4m3").T @ mxq(z, 0, "e4m3") + mxq(f64(w3), 0, "e4m3").T @ mxq(z2, 0, "e4m3")
    b1 = h[np.arange(N)[:, None], runs(n4, N)]
    b2 = h[np.arange(N)[:, None], runs(n5, N)]
    b3 = h[np.arange(N)[:, None], runs(n6, N)]
    return np.maximum(np.maximum(b1, b2), b3) - (0.5 * (np.maximum(np.minimum(b1, b2), np.minimum(np.maximum(b1, b2), b3))))

@@ -1,0 +1,246 @@
+from contextlib import ExitStack
+
+import concourse.mybir as mybir
+from concourse.masks import make_identity
+
+F32 = mybir.dt.float32
+BF16 = mybir.dt.bfloat16
+I32 = mybir.dt.int32
+U32 = mybir.dt.uint32
+U16 = mybir.dt.uint16
+U8 = mybir.dt.uint8
+FP8X4 = mybir.dt.float8_e4m3fn_x4
+ALU = mybir.AluOpType
+ACT = mybir.ActivationFunctionType
+
+P = 128
+PACK = 4
+T, S = 2048, 512
+BLK = S // P
+FLOPS = 3 * 2 * 512 * 512 * 512
+
+
+def tile_picked_joinharmrangetop2_none_p_kernel(
+    tc, x_words, x_scales, w1, gn, gm, w2, w3, offs, n1, n2, n3, n4, n5, n6, out
+):
+    nc = tc.nc
+    with ExitStack() as ctx:
+        lists = ctx.enter_context(tc.tile_pool(name="lists", bufs=1))
+        keep = ctx.enter_context(tc.tile_pool(name="keep", bufs=1))
+        ring = ctx.enter_context(tc.tile_pool(name="ring", bufs=2))
+        ps_mm = ctx.enter_context(tc.psum_pool(name="ps_mm", bufs=2))
+        ps_fw = ctx.enter_context(tc.psum_pool(name="ps_fw", bufs=3))
+        ps_bk = ctx.enter_context(tc.psum_pool(name="ps_bk", bufs=3))
+
+        def load_list(src, name):
+            tl = lists.tile([P, S // 16], U16, name=name)
+            nc.sync.dma_start(tl[:], src)
+            return tl
+
+        def load_weight(w, c0, c1, name):
+            raw = keep.tile([P, PACK, c1 - c0], F32, name=name)
+            nc.sync.dma_start(out=raw[:], in_=w.rearrange("(p j) c -> p j c", j=PACK)[:, :, c0:c1])
+            return raw
+
+        def deal(copy, grouped, raw, c0, c1):
+            copy(
+                out=grouped[:, :, c0 // PACK : c1 // PACK, :].rearrange("p t m j -> p m t j"),
+                in_=raw[:].rearrange("p j (m t) -> p m t j", t=PACK),
+            )
+
+        def mx_tiles(name):
+            codes = keep.tile([P, S], U32, name=name + "_codes", align_bytes=64)
+            scales = keep.tile([P, S], U8, name=name + "_scales", align_bytes=64)
+            return codes, scales
+
+        def quantize(mx, grouped_flat, c0, c1):
+            nc.vector.quantize_mx(
+                out=mx[0][:, c0:c1].bitcast(FP8X4), scales=mx[1][:, c0:c1], in_=grouped_flat[:, PACK * c0 : PACK * c1]
+            )
+
+        def product(bank, w_mx, t, x_mx, start, stop):
+            cols = slice(t * P, (t + 1) * P)
+            nc.tensor.matmul_mx(
+                out=bank[:], lhsT=w_mx[0][:, cols].bitcast(FP8X4), lhsT_scale=w_mx[1][:, cols],
+                rhs=x_mx[0][:].bitcast(FP8X4), rhs_scale=x_mx[1][:], start=start, stop=stop,
+            )
+
+        def turn_sum(pool, terms, name):
+            bank = pool.tile([P, S], F32, name=name)
+            for b in range(BLK):
+                cols = slice(b * P, (b + 1) * P)
+                for i, term in enumerate(terms):
+                    nc.tensor.matmul(
+                        bank[:, cols], term[:, cols], ident[:], is_transpose=True,
+                        start=(i == 0), stop=(i == len(terms) - 1),
+                    )
+            return bank
+
+        xs = keep.tile([P, T], U8, name="xs")
+        nc.vector.memset(xs[:].bitcast(I32), 0)
+        warm = keep.tile([P, 2], F32, name="warm")
+        nc.vector.memset(warm[:, 0:1], 1.0)
+        nc.scalar.activation(warm[:, 1:2], warm[:, 0:1], ACT.Abs_reciprocal_sqrt)
+        offs_t = load_list(offs, "offs_t")
+        xw = keep.tile([P, T], U32, name="xw")
+        nc.sync.dma_start(out=xw[:].bitcast(I32), in_=x_words[0].rearrange("p n t -> p (n t)").bitcast(I32))
+        for q in range(4):
+            nc.scalar.dma_start(
+                out=xs[32 * q : 32 * q + 4, :].bitcast(I32), in_=x_scales[0, 4 * q : 4 * q + 4, :].bitcast(I32)
+            )
+        w1_raw = [load_weight(w1, 256 * u, 256 * (u + 1), f"w1_raw{u}") for u in range(2)]
+        n1_t = load_list(n1, "n1_t")
+        gn_t = keep.tile([P, PACK], F32, name="gn_t")
+        nc.sync.dma_start(out=gn_t[:], in_=gn.rearrange("(p t) o -> p (t o)", t=PACK))
+        gm_t = keep.tile([P, PACK], F32, name="gm_t")
+        nc.sync.dma_start(out=gm_t[:], in_=gm.rearrange("(p t) o -> p (t o)", t=PACK))
+        n2_t = load_list(n2, "n2_t")
+        n3_t = load_list(n3, "n3_t")
+        w2_raw = load_weight(w2, 0, S, "w2_raw")
+        w3_raw = load_weight(w3, 0, S, "w3_raw")
+        n4_t = load_list(n4, "n4_t")
+        n5_t = load_list(n5, "n5_t")
+        n6_t = load_list(n6, "n6_t")
+
+        ywin = [keep.tile([P, 2 * S], F32, name=f"ywin{t}") for t in range(PACK)]
+        for t in range(PACK):
+            nc.gpsimd.memset(ywin[t][:, S:], 0.0)
+        ident = keep.tile([P, P], F32, name="ident")
+        make_identity(nc, ident[:])
+
+        x_mx = mx_tiles("x")
+        w1_b = keep.tile([P, PACK, P, PACK], BF16, name="w1_b", align_bytes=64)
+        deal(nc.scalar.copy, w1_b, w1_raw[0], 0, 256)
+        nc.vector.tensor_copy(x_mx[0][:], xw[:].indirect(offs_t[:]))
+        nc.vector.tensor_copy(x_mx[1][:], xs[:].indirect(offs_t[:]))
+        deal(nc.vector.tensor_copy, w1_b, w1_raw[1], 256, 512)
+        w1_mx = mx_tiles("w1")
+        w1_flat = w1_b[:].rearrange("p t m j -> p (t m j)")
+        for t in range(PACK):
+            quantize(w1_mx, w1_flat, t * P, (t + 1) * P)
+
+        yplain = [keep.tile([P, S], F32, name=f"yplain{t}") for t in range(PACK)]
+        for t in range(PACK):
+            bank = ps_mm.tile([P, S], F32, name="mm")
+            product(bank, w1_mx, t, x_mx, True, True)
+            nc.scalar.copy(ywin[t][:, :S], bank[:])
+            nc.sync.dma_start(out=yplain[t][:], in_=ywin[t][:, :S])
+
+        hwin = [keep.tile([P, 2 * S], F32, name=f"hwin{t}") for t in range(PACK)]
+        pa = [keep.tile([P, S], F32, name=f"pa{t}") for t in range(PACK)]
+        recip = keep.tile([P, PACK, S], F32, name="recip")
+        for t in range(PACK):
+            nc.vector.tensor_copy(pa[t][:], ywin[t][:].indirect(n1_t[:]))
+
+        def denominator(t):
+            ysq = hwin[t][:, S:]
+            nc.scalar.activation(ysq, ywin[t][:, :S], ACT.Square)
+            pasq = ring.tile([P, S], F32, name="pasq")
+            nc.scalar.activation(pasq[:], pa[t][:], ACT.Square)
+            den = turn_sum(ps_fw, [ysq, pasq[:]], "fw")
+            root = ring.tile([P, S], F32, name="root")
+            nc.scalar.activation(root[:], den[:], ACT.Abs_reciprocal_sqrt, scale=0.5, bias=0.25)
+            back = turn_sum(ps_bk, [root[:]], "bk")
+            nc.scalar.activation(recip[:, t, :], back[:], ACT.Square)
+
+        z2_rows = keep.tile([P, PACK, S], BF16, name="z2_rows")
+
+        def spread(t):
+            d1 = ring.tile([P, S], F32, name="d1")
+            d2 = ring.tile([P, S], F32, name="d2")
+            nc.vector.tensor_tensor(d1[:], ywin[t][:].indirect(n2_t[:]), yplain[t][:], ALU.subtract)
+            nc.vector.tensor_tensor(d2[:], ywin[t][:].indirect(n3_t[:]), yplain[t][:], ALU.subtract)
+            low = ring.tile([P, S], F32, name="low")
+            high = ring.tile([P, S], F32, name="high")
+            nc.vector.scalar_tensor_tensor(low[:], d1[:], 0.0, d2[:], ALU.min, ALU.min)
+            nc.vector.scalar_tensor_tensor(high[:], d1[:], 0.0, d2[:], ALU.max, ALU.max)
+            neg = ring.tile([P, S], F32, name="neg")
+            nc.scalar.activation(neg[:], low[:], ACT.Copy, scale=-1.0)
+            total = turn_sum(ps_fw, [yplain[t][:], high[:], high[:], neg[:]], "fw")
+            half = ring.tile([P, S], F32, name="half")
+            nc.scalar.activation(half[:], total[:], ACT.Copy, scale=0.5)
+            back = turn_sum(ps_bk, [half[:]], "bk")
+            nc.scalar.activation(z2_rows[:, t, :], back[:], ACT.Copy, scale=gm_t[:, t : t + 1])
+
+        w2_b = keep.tile([P, PACK, P, PACK], BF16, name="w2_b", align_bytes=64)
+        w3_b = keep.tile([P, PACK, P, PACK], BF16, name="w3_b", align_bytes=64)
+        denominator(0)
+        denominator(1)
+        spread(0)
+        denominator(2)
+        spread(1)
+        denominator(3)
+        spread(2)
+        deal(nc.scalar.copy, w2_b, w2_raw, 0, S)
+        spread(3)
+
+        num = keep.tile([P, PACK, S], F32, name="num")
+        for t in range(PACK):
+            nc.vector.scalar_tensor_tensor(
+                num[:, t, :], pa[t][:], gn_t[:, t : t + 1], yplain[t][:], ALU.mult, ALU.mult
+            )
+        deal(nc.vector.tensor_copy, w3_b, w3_raw, 0, S)
+        z_b = keep.tile([P, S, PACK], BF16, name="z_b", align_bytes=64)
+        nc.vector.tensor_tensor(
+            z_b[:].rearrange("p (c i) t -> p c t i", i=2),
+            num[:].rearrange("p t (c i) -> p c t i", i=2),
+            recip[:].rearrange("p t (c i) -> p c t i", i=2),
+            ALU.mult,
+        )
+        w2_mx, w3_mx, z_mx, z2_mx = mx_tiles("w2"), mx_tiles("w3"), mx_tiles("z"), mx_tiles("z2")
+        quantize(w3_mx, w3_b[:].rearrange("p t m j -> p (t m j)"), 0, S)
+        quantize(w2_mx, w2_b[:].rearrange("p t m j -> p (t m j)"), 0, S)
+        quantize(z_mx, z_b[:].rearrange("p c t -> p (c t)"), 0, S)
+        z2_b = keep.tile([P, S, PACK], BF16, name="z2_b", align_bytes=64)
+        nc.vector.tensor_copy(
+            z2_b[:].rearrange("p (c i) t -> p c t i", i=4), z2_rows[:].rearrange("p t (c i) -> p c t i", i=4)
+        )
+        quantize(z2_mx, z2_b[:].rearrange("p c t -> p (c t)"), 0, S)
+
+        for t in range(PACK):
+            bank = ps_mm.tile([P, S], F32, name="mm")
+            product(bank, w2_mx, t, z_mx, True, False)
+            product(bank, w3_mx, t, z2_mx, False, True)
+            nc.scalar.copy(hwin[t][:, :S], bank[:])
+
+        out_rows = out.rearrange("(p t) j -> p t j", t=PACK)
+
+        def first_steps(t, c0, c1, tag):
+            n = c1 - c0
+            k = slice(c0 // 16, c1 // 16)
+            b1 = ring.tile([P, n], F32, name="b1" + tag)
+            nc.vector.tensor_copy(b1[:], hwin[t][:].indirect(n4_t[:, k]))
+            x = ring.tile([P, n], F32, name="x" + tag)
+            nc.vector.tensor_tensor(x[:], hwin[t][:].indirect(n5_t[:, k]), b1[:], ALU.subtract)
+            gap = ring.tile([P, n], F32, name="gap" + tag)
+            nc.scalar.activation(gap[:], x[:], ACT.Abs, scale=0.5)
+            hi = ring.tile([P, n], F32, name="hi" + tag)
+            nc.vector.scalar_tensor_tensor(hi[:], x[:], 0.0, b1[:], ALU.max, ALU.add)
+            g = ring.tile([P, n], F32, name="g" + tag)
+            nc.vector.tensor_tensor(g[:], hwin[t][:].indirect(n6_t[:, k]), hi[:], ALU.subtract)
+            q = ring.tile([P, n], F32, name="q" + tag)
+            nc.vector.scalar_tensor_tensor(q[:], g[:], -0.5, gap[:], ALU.mult, ALU.min)
+            return hi, g, q
+
+        for t in range(PACK - 1):
+            hi, g, q = first_steps(t, 0, S, "")
+            rg = ring.tile([P, S], F32, name="rg")
+            nc.scalar.activation(rg[:], g[:], ACT.Relu, scale=2.0)
+            rq = ring.tile([P, S], F32, name="rq")
+            nc.scalar.activation(rq[:], q[:], ACT.Relu, scale=2.0)
+            total = turn_sum(ps_fw, [hi[:], rg[:], rq[:]], "fw")
+            half = ring.tile([P, S], F32, name="half")
+            nc.scalar.activation(half[:], total[:], ACT.Copy, scale=0.5)
+            back = turn_sum(ps_bk, [half[:]], "bk")
+            res = ring.tile([P, S], F32, name="res")
+            nc.scalar.copy(res[:], back[:])
+            nc.sync.dma_start(out=out_rows[:, t, :], in_=res[:])
+        t = PACK - 1
+        for c0 in (0, S // 2):
+            c1 = c0 + S // 2
+            hi, g, q = first_steps(t, c0, c1, "h")
+            s = ring.tile([P, S // 2], F32, name="sh")
+            nc.vector.tensor_tensor(s[:], q[:], g[:], ALU.max)
+            res = ring.tile([P, S // 2], F32, name="resh")
+            nc.vector.scalar_tensor_tensor(res[:], hi[:], 0.5, s[:], ALU.mult, ALU.add)
+            nc.sync.dma_start(out=out_rows[:, t, c0:c1], in_=res[:])

@@ -29,28 +29,28 @@ def tile_picked_joinharmrangetop2_none_p_kernel(
         keep = ctx.enter_context(tc.tile_pool(name="keep", bufs=1))
         ring = ctx.enter_context(tc.tile_pool(name="ring", bufs=2))
         ps_mm = ctx.enter_context(tc.psum_pool(name="ps_mm", bufs=2))
-        ps_fw = ctx.enter_context(tc.psum_pool(name="ps_fw", bufs=3))
-        ps_bk = ctx.enter_context(tc.psum_pool(name="ps_bk", bufs=3))
+        ps_fw = ctx.enter_context(tc.psum_pool(name="ps_fw", bufs=4))
+        ps_bk = ctx.enter_context(tc.psum_pool(name="ps_bk", bufs=2))
 
         def load_list(src, name):
             tl = lists.tile([P, S // 16], U16, name=name)
             nc.sync.dma_start(tl[:], src)
             return tl
 
-        def load_weight(w, c0, c1, name):
-            raw = keep.tile([P, PACK, c1 - c0], F32, name=name)
-            nc.sync.dma_start(out=raw[:], in_=w.rearrange("(p j) c -> p j c", j=PACK)[:, :, c0:c1])
+        def load_weight(w, name):
+            raw = keep.tile([P, PACK, S], F32, name=name)
+            nc.sync.dma_start(out=raw[:], in_=w.rearrange("(p j) c -> p j c", j=PACK))
             return raw
 
         def deal(copy, grouped, raw, c0, c1):
             copy(
                 out=grouped[:, :, c0 // PACK : c1 // PACK, :].rearrange("p t m j -> p m t j"),
-                in_=raw[:].rearrange("p j (m t) -> p m t j", t=PACK),
+                in_=raw[:, :, c0:c1].rearrange("p j (m t) -> p m t j", t=PACK),
             )
 
-        def mx_tiles(name):
-            codes = keep.tile([P, S], U32, name=name + "_codes", align_bytes=64)
-            scales = keep.tile([P, S], U8, name=name + "_scales", align_bytes=64)
+        def mx_tiles(name, width=S):
+            codes = keep.tile([P, width], U32, name=name + "_codes", align_bytes=64)
+            scales = keep.tile([P, width], U8, name=name + "_scales", align_bytes=64)
             return codes, scales
 
         def quantize(mx, grouped_flat, c0, c1):
@@ -58,11 +58,11 @@ def tile_picked_joinharmrangetop2_none_p_kernel(
                 out=mx[0][:, c0:c1].bitcast(FP8X4), scales=mx[1][:, c0:c1], in_=grouped_flat[:, PACK * c0 : PACK * c1]
             )
 
-        def product(bank, w_mx, t, x_mx, start, stop):
+        def product(bank, w_mx, t, x_mx, c0, c1, start, stop):
             cols = slice(t * P, (t + 1) * P)
             nc.tensor.matmul_mx(
-                out=bank[:], lhsT=w_mx[0][:, cols].bitcast(FP8X4), lhsT_scale=w_mx[1][:, cols],
-                rhs=x_mx[0][:].bitcast(FP8X4), rhs_scale=x_mx[1][:], start=start, stop=stop,
+                out=bank[:, c0:c1], lhsT=w_mx[0][:, cols].bitcast(FP8X4), lhsT_scale=w_mx[1][:, cols],
+                rhs=x_mx[0][:, c0:c1].bitcast(FP8X4), rhs_scale=x_mx[1][:, c0:c1], start=start, stop=stop,
             )
 
         def turn_sum(pool, terms, name):
@@ -82,22 +82,22 @@ def tile_picked_joinharmrangetop2_none_p_kernel(
         nc.vector.memset(warm[:, 0:1], 1.0)
         nc.scalar.activation(warm[:, 1:2], warm[:, 0:1], ACT.Abs_reciprocal_sqrt)
         offs_t = load_list(offs, "offs_t")
-        xw = keep.tile([P, T], U32, name="xw")
-        nc.sync.dma_start(out=xw[:].bitcast(I32), in_=x_words[0].rearrange("p n t -> p (n t)").bitcast(I32))
+        w1_raw = load_weight(w1, "w1_raw")
         for q in range(4):
             nc.scalar.dma_start(
                 out=xs[32 * q : 32 * q + 4, :].bitcast(I32), in_=x_scales[0, 4 * q : 4 * q + 4, :].bitcast(I32)
             )
-        w1_raw = [load_weight(w1, 256 * u, 256 * (u + 1), f"w1_raw{u}") for u in range(2)]
+        xw = keep.tile([P, T], U32, name="xw")
+        nc.sync.dma_start(out=xw[:].bitcast(I32), in_=x_words[0].rearrange("p n t -> p (n t)").bitcast(I32))
         n1_t = load_list(n1, "n1_t")
+        w2_raw = load_weight(w2, "w2_raw")
         gn_t = keep.tile([P, PACK], F32, name="gn_t")
         nc.sync.dma_start(out=gn_t[:], in_=gn.rearrange("(p t) o -> p (t o)", t=PACK))
         gm_t = keep.tile([P, PACK], F32, name="gm_t")
         nc.sync.dma_start(out=gm_t[:], in_=gm.rearrange("(p t) o -> p (t o)", t=PACK))
         n2_t = load_list(n2, "n2_t")
         n3_t = load_list(n3, "n3_t")
-        w2_raw = load_weight(w2, 0, S, "w2_raw")
-        w3_raw = load_weight(w3, 0, S, "w3_raw")
+        w3_raw = load_weight(w3, "w3_raw")
         n4_t = load_list(n4, "n4_t")
         n5_t = load_list(n5, "n5_t")
         n6_t = load_list(n6, "n6_t")
@@ -110,19 +110,23 @@ def tile_picked_joinharmrangetop2_none_p_kernel(
 
         x_mx = mx_tiles("x")
         w1_b = keep.tile([P, PACK, P, PACK], BF16, name="w1_b", align_bytes=64)
-        deal(nc.scalar.copy, w1_b, w1_raw[0], 0, 256)
-        nc.vector.tensor_copy(x_mx[0][:], xw[:].indirect(offs_t[:]))
+        deal(nc.scalar.copy, w1_b, w1_raw, 0, 192)
+        deal(nc.vector.tensor_copy, w1_b, w1_raw, 192, S)
         nc.vector.tensor_copy(x_mx[1][:], xs[:].indirect(offs_t[:]))
-        deal(nc.vector.tensor_copy, w1_b, w1_raw[1], 256, 512)
         w1_mx = mx_tiles("w1")
-        w1_flat = w1_b[:].rearrange("p t m j -> p (t m j)")
-        for t in range(PACK):
-            quantize(w1_mx, w1_flat, t * P, (t + 1) * P)
+        quantize(w1_mx, w1_b[:].rearrange("p t m j -> p (t m j)"), 0, S)
+        for c0 in (0, S // 2):
+            nc.vector.tensor_copy(
+                x_mx[0][:, c0 : c0 + S // 2], xw[:].indirect(offs_t[:, c0 // 16 : (c0 + S // 2) // 16])
+            )
+        w2_b = keep.tile([P, PACK, P, PACK], BF16, name="w2_b", align_bytes=64)
+        deal(nc.vector.tensor_copy, w2_b, w2_raw, 0, S)
 
         yplain = [keep.tile([P, S], F32, name=f"yplain{t}") for t in range(PACK)]
         for t in range(PACK):
             bank = ps_mm.tile([P, S], F32, name="mm")
-            product(bank, w1_mx, t, x_mx, True, True)
+            for c0 in (0, S // 2):
+                product(bank, w1_mx, t, x_mx, c0, c0 + S // 2, True, True)
             nc.scalar.copy(ywin[t][:, :S], bank[:])
             nc.sync.dma_start(out=yplain[t][:], in_=ywin[t][:, :S])
 
@@ -137,49 +141,60 @@ def tile_picked_joinharmrangetop2_none_p_kernel(
             nc.scalar.activation(ysq, ywin[t][:, :S], ACT.Square)
             pasq = ring.tile([P, S], F32, name="pasq")
             nc.scalar.activation(pasq[:], pa[t][:], ACT.Square)
-            den = turn_sum(ps_fw, [ysq, pasq[:]], "fw")
+            den = turn_sum(ps_fw, [pasq[:], ysq], "fw")
             root = ring.tile([P, S], F32, name="root")
             nc.scalar.activation(root[:], den[:], ACT.Abs_reciprocal_sqrt, scale=0.5, bias=0.25)
             back = turn_sum(ps_bk, [root[:]], "bk")
             nc.scalar.activation(recip[:, t, :], back[:], ACT.Square)
 
-        z2_rows = keep.tile([P, PACK, S], BF16, name="z2_rows")
+        z2_rows = keep.tile([P, PACK, S], BF16, name="z2_rows", align_bytes=64)
+        num = keep.tile([P, PACK, S], F32, name="num")
+        diffs = keep.tile([P, PACK, S], F32, name="diffs")
+        lows = [keep.tile([P, S], F32, name=f"low{t}", align_bytes=64) for t in range(PACK)]
+        highs = [keep.tile([P, S], F32, name=f"high{t}") for t in range(PACK)]
+
+        def diff(t, i):
+            slot = 2 * t + i
+            return diffs[:, slot, :] if slot < PACK else num[:, slot - PACK, :]
+
+        def fetch_diff(t, i):
+            nc.vector.tensor_tensor(diff(t, i), ywin[t][:].indirect((n2_t, n3_t)[i][:]), yplain[t][:], ALU.subtract)
+
+        def extreme(t, dst, op):
+            nc.vector.scalar_tensor_tensor(dst[t][:], diff(t, 0), 0.0, diff(t, 1), op, op)
 
         def spread(t):
-            d1 = ring.tile([P, S], F32, name="d1")
-            d2 = ring.tile([P, S], F32, name="d2")
-            nc.vector.tensor_tensor(d1[:], ywin[t][:].indirect(n2_t[:]), yplain[t][:], ALU.subtract)
-            nc.vector.tensor_tensor(d2[:], ywin[t][:].indirect(n3_t[:]), yplain[t][:], ALU.subtract)
-            low = ring.tile([P, S], F32, name="low")
-            high = ring.tile([P, S], F32, name="high")
-            nc.vector.scalar_tensor_tensor(low[:], d1[:], 0.0, d2[:], ALU.min, ALU.min)
-            nc.vector.scalar_tensor_tensor(high[:], d1[:], 0.0, d2[:], ALU.max, ALU.max)
-            neg = ring.tile([P, S], F32, name="neg")
-            nc.scalar.activation(neg[:], low[:], ACT.Copy, scale=-1.0)
-            total = turn_sum(ps_fw, [yplain[t][:], high[:], high[:], neg[:]], "fw")
+            neg = highs[t - 1] if t else ring.tile([P, S], F32, name="root")
+            nc.scalar.activation(neg[:], lows[t][:], ACT.Copy, scale=-1.0)
+            total = turn_sum(ps_fw, [neg[:], yplain[t][:], highs[t][:], highs[t][:]], "fw")
             half = ring.tile([P, S], F32, name="half")
             nc.scalar.activation(half[:], total[:], ACT.Copy, scale=0.5)
             back = turn_sum(ps_bk, [half[:]], "bk")
             nc.scalar.activation(z2_rows[:, t, :], back[:], ACT.Copy, scale=gm_t[:, t : t + 1])
 
-        w2_b = keep.tile([P, PACK, P, PACK], BF16, name="w2_b", align_bytes=64)
-        w3_b = keep.tile([P, PACK, P, PACK], BF16, name="w3_b", align_bytes=64)
-        denominator(0)
-        denominator(1)
-        spread(0)
-        denominator(2)
-        spread(1)
-        denominator(3)
-        spread(2)
-        deal(nc.scalar.copy, w2_b, w2_raw, 0, S)
-        spread(3)
-
-        num = keep.tile([P, PACK, S], F32, name="num")
-        for t in range(PACK):
+        def numerator(t):
             nc.vector.scalar_tensor_tensor(
                 num[:, t, :], pa[t][:], gn_t[:, t : t + 1], yplain[t][:], ALU.mult, ALU.mult
             )
-        deal(nc.vector.tensor_copy, w3_b, w3_raw, 0, S)
+
+        for t in range(PACK):
+            denominator(t)
+        fetch_diff(0, 0)
+        for t in range(PACK):
+            fetch_diff(t, 1)
+            if t + 1 < PACK:
+                fetch_diff(t + 1, 0)
+            else:
+                numerator(0)
+            extreme(t, lows, ALU.min)
+            extreme(t, highs, ALU.max)
+        for t in range(PACK):
+            spread(t)
+        w3_b = keep.tile([P, PACK, P, PACK], BF16, name="low0", align_bytes=64)
+        for t in range(PACK):
+            deal(nc.scalar.copy, w3_b, w3_raw, t * P, (t + 1) * P)
+        for t in range(1, PACK):
+            numerator(t)
         z_b = keep.tile([P, S, PACK], BF16, name="z_b", align_bytes=64)
         nc.vector.tensor_tensor(
             z_b[:].rearrange("p (c i) t -> p c t i", i=2),
@@ -187,60 +202,101 @@ def tile_picked_joinharmrangetop2_none_p_kernel(
             recip[:].rearrange("p t (c i) -> p c t i", i=2),
             ALU.mult,
         )
-        w2_mx, w3_mx, z_mx, z2_mx = mx_tiles("w2"), mx_tiles("w3"), mx_tiles("z"), mx_tiles("z2")
-        quantize(w3_mx, w3_b[:].rearrange("p t m j -> p (t m j)"), 0, S)
-        quantize(w2_mx, w2_b[:].rearrange("p t m j -> p (t m j)"), 0, S)
+        z_mx, z2_mx = mx_tiles("z"), mx_tiles("z2")
+        w_flat = [w[:].rearrange("p t m j -> p (t m j)") for w in (w2_b, w3_b)]
+        first_mx = [mx_tiles("w2_first", P), mx_tiles("w3_first", P)]
+        for i in range(2):
+            quantize(first_mx[i], w_flat[i], 0, P)
         quantize(z_mx, z_b[:].rearrange("p c t -> p (c t)"), 0, S)
         z2_b = keep.tile([P, S, PACK], BF16, name="z2_b", align_bytes=64)
-        nc.vector.tensor_copy(
-            z2_b[:].rearrange("p (c i) t -> p c t i", i=4), z2_rows[:].rearrange("p t (c i) -> p c t i", i=4)
-        )
-        quantize(z2_mx, z2_b[:].rearrange("p c t -> p (c t)"), 0, S)
+        halves = [(0, S // 2), (S // 2, S)]
+        for c0, c1 in halves:
+            nc.vector.tensor_copy(
+                z2_b[:, c0:c1, :].rearrange("p (c i) t -> p c t i", i=4),
+                z2_rows[:, :, c0:c1].rearrange("p t (c i) -> p c t i", i=4),
+            )
+        for c0, c1 in halves:
+            quantize(z2_mx, z2_b[:].rearrange("p c t -> p (c t)"), c0, c1)
+        late_codes = keep.tile([P, 2, S], U32, name="z2_rows", align_bytes=64)
+        late_scales = keep.tile([P, 2, S], U8, name="late_scales", align_bytes=64)
+        late_mx = [(late_codes[:, i, :], late_scales[:, i, :]) for i in range(2)]
+        for c0, c1 in ((P, 2 * P), (2 * P, S)):
+            for i in range(2):
+                quantize(late_mx[i], w_flat[i], c0, c1)
 
-        for t in range(PACK):
+        for (c0, c1), copy in zip(halves, (nc.scalar.copy, nc.vector.tensor_copy)):
+            bank = ps_bk.tile([P, S], F32, name="bk")
+            product(bank, first_mx[1], 0, z2_mx, c0, c1, True, False)
+            product(bank, first_mx[0], 0, z_mx, c0, c1, False, True)
+            copy(hwin[0][:, c0:c1], bank[:, c0:c1])
+        for t in range(1, PACK):
             bank = ps_mm.tile([P, S], F32, name="mm")
-            product(bank, w2_mx, t, z_mx, True, False)
-            product(bank, w3_mx, t, z2_mx, False, True)
+            product(bank, late_mx[1], t, z2_mx, 0, S, True, False)
+            product(bank, late_mx[0], t, z_mx, 0, S, False, True)
             nc.scalar.copy(hwin[t][:, :S], bank[:])
 
         out_rows = out.rearrange("(p t) j -> p t j", t=PACK)
 
-        def first_steps(t, c0, c1, tag):
-            n = c1 - c0
-            k = slice(c0 // 16, c1 // 16)
-            b1 = ring.tile([P, n], F32, name="b1" + tag)
-            nc.vector.tensor_copy(b1[:], hwin[t][:].indirect(n4_t[:, k]))
-            x = ring.tile([P, n], F32, name="x" + tag)
-            nc.vector.tensor_tensor(x[:], hwin[t][:].indirect(n5_t[:, k]), b1[:], ALU.subtract)
-            gap = ring.tile([P, n], F32, name="gap" + tag)
-            nc.scalar.activation(gap[:], x[:], ACT.Abs, scale=0.5)
-            hi = ring.tile([P, n], F32, name="hi" + tag)
-            nc.vector.scalar_tensor_tensor(hi[:], x[:], 0.0, b1[:], ALU.max, ALU.add)
-            g = ring.tile([P, n], F32, name="g" + tag)
-            nc.vector.tensor_tensor(g[:], hwin[t][:].indirect(n6_t[:, k]), hi[:], ALU.subtract)
-            q = ring.tile([P, n], F32, name="q" + tag)
-            nc.vector.scalar_tensor_tensor(q[:], g[:], -0.5, gap[:], ALU.mult, ALU.min)
-            return hi, g, q
+        vals = [dict() for t in range(PACK)]
 
-        for t in range(PACK - 1):
-            hi, g, q = first_steps(t, 0, S, "")
-            rg = ring.tile([P, S], F32, name="rg")
-            nc.scalar.activation(rg[:], g[:], ACT.Relu, scale=2.0)
-            rq = ring.tile([P, S], F32, name="rq")
-            nc.scalar.activation(rq[:], q[:], ACT.Relu, scale=2.0)
-            total = turn_sum(ps_fw, [hi[:], rg[:], rq[:]], "fw")
+        def fresh(t, name):
+            tl = keep.tile([P, S], F32, name=f"{name}{t}")
+            vals[t][name] = tl
+            return tl[:]
+
+        def step_b(t):
+            nc.vector.tensor_copy(fresh(t, "b1"), hwin[t][:].indirect(n4_t[:]))
+
+        def step_x(t):
+            nc.vector.tensor_tensor(fresh(t, "x"), hwin[t][:].indirect(n5_t[:]), vals[t]["b1"][:], ALU.subtract)
+
+        def step_a(t):
+            gap = ring.tile([P, S], F32, name="gap" if t < 2 else "pasq")
+            vals[t]["gap"] = gap
+            nc.scalar.activation(gap[:], vals[t]["x"][:], ACT.Abs)
+
+        def step_h(t):
+            nc.vector.scalar_tensor_tensor(fresh(t, "hi"), vals[t]["x"][:], 0.0, vals[t]["b1"][:], ALU.max, ALU.add)
+
+        def step_g(t):
+            nc.vector.tensor_tensor(fresh(t, "g"), hwin[t][:].indirect(n6_t[:]), vals[t]["hi"][:], ALU.subtract)
+
+        def finish_turned(t):
+            v = vals[t]
+            under = turn_sum(ps_fw, [v["g"][:], v["gap"][:]], "fw")
+            ag = ring.tile([P, S], F32, name="pasq")
+            nc.scalar.activation(ag[:], v["g"][:], ACT.Abs, scale=3.0)
+            ru = ring.tile([P, S], F32, name="root")
+            nc.scalar.activation(ru[:], under[:], ACT.Relu, scale=-2.0)
+            total = turn_sum(ps_fw, [ag[:], v["hi"][:], v["hi"][:], v["g"][:]], "fw")
             half = ring.tile([P, S], F32, name="half")
-            nc.scalar.activation(half[:], total[:], ACT.Copy, scale=0.5)
-            back = turn_sum(ps_bk, [half[:]], "bk")
+            nc.scalar.activation(half[:], total[:], ACT.Copy, scale=-1.0)
+            back = turn_sum(ps_bk, [half[:], ru[:]], "bk")
             res = ring.tile([P, S], F32, name="res")
-            nc.scalar.copy(res[:], back[:])
+            nc.scalar.activation(res[:], back[:], ACT.Copy, scale=-0.25)
             nc.sync.dma_start(out=out_rows[:, t, :], in_=res[:])
-        t = PACK - 1
-        for c0 in (0, S // 2):
-            c1 = c0 + S // 2
-            hi, g, q = first_steps(t, c0, c1, "h")
-            s = ring.tile([P, S // 2], F32, name="sh")
-            nc.vector.tensor_tensor(s[:], q[:], g[:], ALU.max)
-            res = ring.tile([P, S // 2], F32, name="resh")
-            nc.vector.scalar_tensor_tensor(res[:], hi[:], 0.5, s[:], ALU.mult, ALU.add)
-            nc.sync.dma_start(out=out_rows[:, t, c0:c1], in_=res[:])
+
+        def step_q(t):
+            v = vals[t]
+            nc.vector.scalar_tensor_tensor(v["b1"][:], v["g"][:], -1.0, v["gap"][:], ALU.mult, ALU.min)
+
+        def step_s(t):
+            v = vals[t]
+            nc.vector.scalar_tensor_tensor(v["x"][:], v["b1"][:], 0.5, v["g"][:], ALU.mult, ALU.max)
+
+        def step_r(t, c0, c1):
+            v = vals[t]
+            nc.vector.scalar_tensor_tensor(v["gap"][:, c0:c1], v["hi"][:, c0:c1], 0.5, v["x"][:, c0:c1], ALU.mult, ALU.add)
+            nc.sync.dma_start(out=out_rows[:, t, c0:c1], in_=v["gap"][:, c0:c1])
+
+        for step in (step_b, step_x, step_a, step_h, step_g):
+            step(0)
+            step(1)
+        finish_turned(0)
+        finish_turned(1)
+        for step in (step_b, step_x, step_a, step_h, step_g, step_q, step_s):
+            step(2)
+            step(3)
+        step_r(2, 0, S)
+        step_r(3, 0, S // 2)
+        step_r(3, S // 2, S)

@@ -120,7 +120,7 @@ def tile_picked_joinharmrangetop2_none_p_kernel(
                 x_mx[0][:, c0 : c0 + S // 2], xw[:].indirect(offs_t[:, c0 // 16 : (c0 + S // 2) // 16])
             )
         w2_b = keep.tile([P, PACK, P, PACK], BF16, name="w2_b", align_bytes=64)
-        deal(nc.vector.tensor_copy, w2_b, w2_raw, 0, S)
+        deal(nc.vector.tensor_copy, w2_b, w2_raw, 0, 256)
 
         yplain = [keep.tile([P, S], F32, name=f"yplain{t}") for t in range(PACK)]
         for t in range(PACK):
@@ -147,77 +147,80 @@ def tile_picked_joinharmrangetop2_none_p_kernel(
             back = turn_sum(ps_bk, [root[:]], "bk")
             nc.scalar.activation(recip[:, t, :], back[:], ACT.Square)
 
-        z2_rows = keep.tile([P, PACK, S], BF16, name="z2_rows", align_bytes=64)
         num = keep.tile([P, PACK, S], F32, name="num")
-        diffs = keep.tile([P, PACK, S], F32, name="diffs")
-        lows = [keep.tile([P, S], F32, name=f"low{t}", align_bytes=64) for t in range(PACK)]
+        upper = keep.tile([P, PACK, S], F32, name="upper")
+        lower = keep.tile([P, PACK, S], F32, name="lower", align_bytes=64)
+        gm_half = keep.tile([P, 2, PACK], F32, name="gm_half")
+        nc.scalar.activation(gm_half[:, 0, :], gm_t[:], ACT.Copy, scale=0.5)
+        nc.scalar.activation(gm_half[:, 1, :], gm_t[:], ACT.Copy, scale=-0.5)
+        diffs = [[keep.tile([P, S], F32, name=f"diff{t % 2}{i}") for i in range(2)] for t in range(PACK)]
+        lows = [keep.tile([P, S], F32, name=f"low{t % 2}") for t in range(PACK)]
         highs = [keep.tile([P, S], F32, name=f"high{t}") for t in range(PACK)]
-
-        def diff(t, i):
-            slot = 2 * t + i
-            return diffs[:, slot, :] if slot < PACK else num[:, slot - PACK, :]
+        yhalf = [keep.tile([P, S], F32, name=f"yhalf{t}") for t in range(PACK)]
 
         def fetch_diff(t, i):
-            nc.vector.tensor_tensor(diff(t, i), ywin[t][:].indirect((n2_t, n3_t)[i][:]), yplain[t][:], ALU.subtract)
+            nc.vector.tensor_tensor(
+                diffs[t][i][:], ywin[t][:].indirect((n2_t, n3_t)[i][:]), yplain[t][:], ALU.subtract
+            )
 
         def extreme(t, dst, op):
-            nc.vector.scalar_tensor_tensor(dst[t][:], diff(t, 0), 0.0, diff(t, 1), op, op)
-
-        def spread(t):
-            neg = highs[t - 1] if t else ring.tile([P, S], F32, name="root")
-            nc.scalar.activation(neg[:], lows[t][:], ACT.Copy, scale=-1.0)
-            total = turn_sum(ps_fw, [neg[:], yplain[t][:], highs[t][:], highs[t][:]], "fw")
-            half = ring.tile([P, S], F32, name="half")
-            nc.scalar.activation(half[:], total[:], ACT.Copy, scale=0.5)
-            back = turn_sum(ps_bk, [half[:]], "bk")
-            nc.scalar.activation(z2_rows[:, t, :], back[:], ACT.Copy, scale=gm_t[:, t : t + 1])
+            nc.vector.scalar_tensor_tensor(dst[t][:], diffs[t][0][:], 0.0, diffs[t][1][:], op, op)
 
         def numerator(t):
             nc.vector.scalar_tensor_tensor(
                 num[:, t, :], pa[t][:], gn_t[:, t : t + 1], yplain[t][:], ALU.mult, ALU.mult
             )
 
+        w3_b = keep.tile([P, PACK, P, PACK], BF16, name="w3_b", align_bytes=64)
         for t in range(PACK):
             denominator(t)
-        fetch_diff(0, 0)
+            if t >= 0:
+                nc.scalar.activation(yhalf[t][:], ywin[t][:, :S], ACT.Copy, scale=gm_half[:, 0, t : t + 1])
         for t in range(PACK):
+            fetch_diff(t, 0)
             fetch_diff(t, 1)
-            if t + 1 < PACK:
-                fetch_diff(t + 1, 0)
-            else:
-                numerator(0)
-            extreme(t, lows, ALU.min)
+            numerator(t)
             extreme(t, highs, ALU.max)
-        for t in range(PACK):
-            spread(t)
-        w3_b = keep.tile([P, PACK, P, PACK], BF16, name="low0", align_bytes=64)
+            extreme(t, lows, ALU.min)
+            if t >= 0:
+                nc.vector.scalar_tensor_tensor(
+                    upper[:, t, :], highs[t][:], gm_t[:, t : t + 1], yhalf[t][:], ALU.mult, ALU.add
+                )
+            else:
+                total = turn_sum(ps_fw, [highs[t][:], highs[t][:], yplain[t][:]], "fw")
+                turned = ring.tile([P, S], F32, name="half")
+                nc.scalar.copy(turned[:], total[:])
+                back = turn_sum(ps_bk, [turned[:]], "bk")
+                nc.scalar.activation(upper[:, t, :], back[:], ACT.Copy, scale=gm_half[:, 0, t : t + 1])
+            nc.scalar.activation(lower[:, t, :], lows[t][:], ACT.Copy, scale=gm_half[:, 1, t : t + 1])
+        for c0 in range(256, S, P):
+            deal(nc.scalar.copy, w2_b, w2_raw, c0, c0 + P)
         for t in range(PACK):
             deal(nc.scalar.copy, w3_b, w3_raw, t * P, (t + 1) * P)
-        for t in range(1, PACK):
-            numerator(t)
-        z_b = keep.tile([P, S, PACK], BF16, name="z_b", align_bytes=64)
-        nc.vector.tensor_tensor(
-            z_b[:].rearrange("p (c i) t -> p c t i", i=2),
-            num[:].rearrange("p t (c i) -> p c t i", i=2),
-            recip[:].rearrange("p t (c i) -> p c t i", i=2),
-            ALU.mult,
-        )
+
+        def combine(dst, a, b, op, c0, c1):
+            nc.vector.tensor_tensor(
+                dst[:, c0:c1, :].rearrange("p (c i) t -> p c t i", i=2),
+                a[:, :, c0:c1].rearrange("p t (c i) -> p c t i", i=2),
+                b[:, :, c0:c1].rearrange("p t (c i) -> p c t i", i=2),
+                op,
+            )
+
         z_mx, z2_mx = mx_tiles("z"), mx_tiles("z2")
         w_flat = [w[:].rearrange("p t m j -> p (t m j)") for w in (w2_b, w3_b)]
         first_mx = [mx_tiles("w2_first", P), mx_tiles("w3_first", P)]
-        for i in range(2):
-            quantize(first_mx[i], w_flat[i], 0, P)
-        quantize(z_mx, z_b[:].rearrange("p c t -> p (c t)"), 0, S)
+        z_b = keep.tile([P, S, PACK], BF16, name="z_b", align_bytes=64)
         z2_b = keep.tile([P, S, PACK], BF16, name="z2_b", align_bytes=64)
         halves = [(0, S // 2), (S // 2, S)]
-        for c0, c1 in halves:
-            nc.vector.tensor_copy(
-                z2_b[:, c0:c1, :].rearrange("p (c i) t -> p c t i", i=4),
-                z2_rows[:, :, c0:c1].rearrange("p t (c i) -> p c t i", i=4),
-            )
+        combine(z_b, num, recip, ALU.mult, 0, S)
+        for i in range(2):
+            quantize(first_mx[i], w_flat[i], 0, P)
+        combine(z2_b, upper, lower, ALU.add, *halves[0])
+        quantize(z_mx, z_b[:].rearrange("p c t -> p (c t)"), 0, S)
+        combine(z2_b, upper, lower, ALU.add, *halves[1])
         for c0, c1 in halves:
             quantize(z2_mx, z2_b[:].rearrange("p c t -> p (c t)"), c0, c1)
-        late_codes = keep.tile([P, 2, S], U32, name="z2_rows", align_bytes=64)
+        late_codes = keep.tile([P, 2, S], U32, name="lower", align_bytes=64)
         late_scales = keep.tile([P, 2, S], U8, name="late_scales", align_bytes=64)
         late_mx = [(late_codes[:, i, :], late_scales[:, i, :]) for i in range(2)]
         for c0, c1 in ((P, 2 * P), (2 * P, S)):
@@ -237,66 +240,79 @@ def tile_picked_joinharmrangetop2_none_p_kernel(
 
         out_rows = out.rearrange("(p t) j -> p t j", t=PACK)
 
-        vals = [dict() for t in range(PACK)]
+        pieces = [(0, 0, S), (1, 0, S), (2, 0, S), (3, 0, S)]
+        vals = [dict() for u in pieces]
 
-        def fresh(t, name):
-            tl = keep.tile([P, S], F32, name=f"{name}{t}")
-            vals[t][name] = tl
+        def fresh(u, name):
+            tl = keep.tile([P, pieces[u][2] - pieces[u][1]], F32, name=f"{name}{u}")
+            vals[u][name] = tl
             return tl[:]
 
-        def step_b(t):
-            nc.vector.tensor_copy(fresh(t, "b1"), hwin[t][:].indirect(n4_t[:]))
+        def looked_up(u, lst):
+            t, c0, c1 = pieces[u]
+            return hwin[t][:].indirect(lst[:, c0 // 16 : c1 // 16])
 
-        def step_x(t):
-            nc.vector.tensor_tensor(fresh(t, "x"), hwin[t][:].indirect(n5_t[:]), vals[t]["b1"][:], ALU.subtract)
+        def step_b(u):
+            nc.vector.tensor_copy(fresh(u, "b1"), looked_up(u, n4_t))
 
-        def step_a(t):
-            gap = ring.tile([P, S], F32, name="gap" if t < 2 else "pasq")
-            vals[t]["gap"] = gap
-            nc.scalar.activation(gap[:], vals[t]["x"][:], ACT.Abs)
+        def step_x(u):
+            nc.vector.tensor_tensor(fresh(u, "x"), looked_up(u, n5_t), vals[u]["b1"][:], ALU.subtract)
+            nc.scalar.activation(fresh(u, "gap"), vals[u]["x"][:], ACT.Abs, scale=0.5)
 
-        def step_h(t):
-            nc.vector.scalar_tensor_tensor(fresh(t, "hi"), vals[t]["x"][:], 0.0, vals[t]["b1"][:], ALU.max, ALU.add)
+        def step_h(u):
+            nc.vector.scalar_tensor_tensor(fresh(u, "hi"), vals[u]["x"][:], 0.0, vals[u]["b1"][:], ALU.max, ALU.add)
 
-        def step_g(t):
-            nc.vector.tensor_tensor(fresh(t, "g"), hwin[t][:].indirect(n6_t[:]), vals[t]["hi"][:], ALU.subtract)
+        def step_g(u):
+            nc.vector.tensor_tensor(fresh(u, "g"), looked_up(u, n6_t), vals[u]["hi"][:], ALU.subtract)
 
-        def finish_turned(t):
-            v = vals[t]
-            under = turn_sum(ps_fw, [v["g"][:], v["gap"][:]], "fw")
-            ag = ring.tile([P, S], F32, name="pasq")
-            nc.scalar.activation(ag[:], v["g"][:], ACT.Abs, scale=3.0)
-            ru = ring.tile([P, S], F32, name="root")
-            nc.scalar.activation(ru[:], under[:], ACT.Relu, scale=-2.0)
-            total = turn_sum(ps_fw, [ag[:], v["hi"][:], v["hi"][:], v["g"][:]], "fw")
-            half = ring.tile([P, S], F32, name="half")
-            nc.scalar.activation(half[:], total[:], ACT.Copy, scale=-1.0)
-            back = turn_sum(ps_bk, [half[:], ru[:]], "bk")
+        def step_q(u):
+            v = vals[u]
+            nc.vector.scalar_tensor_tensor(v["b1"][:], v["g"][:], -0.5, v["gap"][:], ALU.mult, ALU.min)
+
+        def turn_top(u):
+            v = vals[u]
+            rg = ring.tile([P, S], F32, name="pasq")
+            nc.scalar.activation(rg[:], v["g"][:], ACT.Relu, scale=2.0)
+            top = turn_sum(ps_fw, [rg[:], v["hi"][:]], "fw")
+            v["top"] = ring.tile([P, S], F32, name="half")
+            nc.scalar.activation(v["top"][:], top[:], ACT.Copy, scale=0.5)
+
+        def turn_rest(u):
+            v = vals[u]
+            rest = turn_sum(ps_fw, [v["b1"][:]], "fw")
+            rq = ring.tile([P, S], F32, name="root")
+            nc.scalar.activation(rq[:], rest[:], ACT.Relu)
+            back = turn_sum(ps_bk, [rq[:], v["top"][:]], "bk")
             res = ring.tile([P, S], F32, name="res")
-            nc.scalar.activation(res[:], back[:], ACT.Copy, scale=-0.25)
-            nc.sync.dma_start(out=out_rows[:, t, :], in_=res[:])
+            nc.scalar.copy(res[:], back[:])
+            nc.sync.dma_start(out=out_rows[:, pieces[u][0], :], in_=res[:])
 
-        def step_q(t):
-            v = vals[t]
-            nc.vector.scalar_tensor_tensor(v["b1"][:], v["g"][:], -1.0, v["gap"][:], ALU.mult, ALU.min)
+        def turn_all(u):
+            v = vals[u]
+            rg = ring.tile([P, S], F32, name="pasq")
+            nc.scalar.activation(rg[:], v["g"][:], ACT.Relu, scale=2.0)
+            rq = ring.tile([P, S], F32, name="root")
+            nc.scalar.activation(rq[:], v["b1"][:], ACT.Relu, scale=2.0)
+            total = turn_sum(ps_fw, [rq[:], rg[:], v["hi"][:]], "fw")
+            half = ring.tile([P, S], F32, name="half")
+            nc.scalar.activation(half[:], total[:], ACT.Copy, scale=0.5)
+            back = turn_sum(ps_bk, [half[:]], "bk")
+            res = ring.tile([P, S], F32, name="res")
+            nc.scalar.copy(res[:], back[:])
+            nc.sync.dma_start(out=out_rows[:, pieces[u][0], :], in_=res[:])
 
-        def step_s(t):
-            v = vals[t]
-            nc.vector.scalar_tensor_tensor(v["x"][:], v["b1"][:], 0.5, v["g"][:], ALU.mult, ALU.max)
+        def step_s(u):
+            v = vals[u]
+            nc.vector.tensor_tensor(v["x"][:], v["b1"][:], v["g"][:], ALU.max)
 
-        def step_r(t, c0, c1):
-            v = vals[t]
-            nc.vector.scalar_tensor_tensor(v["gap"][:, c0:c1], v["hi"][:, c0:c1], 0.5, v["x"][:, c0:c1], ALU.mult, ALU.add)
-            nc.sync.dma_start(out=out_rows[:, t, c0:c1], in_=v["gap"][:, c0:c1])
+        def step_r(u):
+            v = vals[u]
+            for c0, c1 in halves if u == PACK - 1 else [(0, S)]:
+                nc.vector.scalar_tensor_tensor(
+                    v["gap"][:, c0:c1], v["hi"][:, c0:c1], 0.5, v["x"][:, c0:c1], ALU.mult, ALU.add
+                )
+                nc.sync.dma_start(out=out_rows[:, u, c0:c1], in_=v["gap"][:, c0:c1])
 
-        for step in (step_b, step_x, step_a, step_h, step_g):
-            step(0)
-            step(1)
-        finish_turned(0)
-        finish_turned(1)
-        for step in (step_b, step_x, step_a, step_h, step_g, step_q, step_s):
-            step(2)
-            step(3)
-        step_r(2, 0, S)
-        step_r(3, 0, S // 2)
-        step_r(3, S // 2, S)
+        steps = dict(b=step_b, x=step_x, h=step_h, g=step_g, q=step_q, s=step_s, r=step_r, t=turn_top, e=turn_rest, a=turn_all)
+        for word in "b0 b1 x0 x1 h0 h1 g0 g1 q0 q1 a0 a1 b2 b3 x2 x3 h2 h3 g2 g3 q2 q3 s2 s3 r2 r3".split():
+            steps[word[0]](int(word[1]))

@@ -77,16 +77,16 @@ def tile_picked_joinharmrangetop2_none_p_kernel(
             return bank
 
         xs = keep.tile([P, T], U8, name="xs")
-        nc.vector.memset(xs[:].bitcast(I32), 0)
+        nc.gpsimd.memset(xs[:].bitcast(I32), 0)
         warm = keep.tile([P, 2], F32, name="warm")
         nc.vector.memset(warm[:, 0:1], 1.0)
-        nc.scalar.activation(warm[:, 1:2], warm[:, 0:1], ACT.Abs_reciprocal_sqrt)
         offs_t = load_list(offs, "offs_t")
         w1_raw = load_weight(w1, "w1_raw")
         for q in range(4):
             nc.scalar.dma_start(
                 out=xs[32 * q : 32 * q + 4, :].bitcast(I32), in_=x_scales[0, 4 * q : 4 * q + 4, :].bitcast(I32)
             )
+        nc.scalar.activation(warm[:, 1:2], warm[:, 0:1], ACT.Abs_reciprocal_sqrt)
         xw = keep.tile([P, T], U32, name="xw")
         nc.sync.dma_start(out=xw[:].bitcast(I32), in_=x_words[0].rearrange("p n t -> p (n t)").bitcast(I32))
         n1_t = load_list(n1, "n1_t")
@@ -110,16 +110,17 @@ def tile_picked_joinharmrangetop2_none_p_kernel(
 
         x_mx = mx_tiles("x")
         w1_b = keep.tile([P, PACK, P, PACK], BF16, name="w1_b", align_bytes=64)
-        deal(nc.scalar.copy, w1_b, w1_raw, 0, 192)
-        deal(nc.vector.tensor_copy, w1_b, w1_raw, 192, S)
+        deal(nc.scalar.copy, w1_b, w1_raw, 0, 256)
         nc.vector.tensor_copy(x_mx[1][:], xs[:].indirect(offs_t[:]))
+        deal(nc.vector.tensor_copy, w1_b, w1_raw, 256, S)
         w1_mx = mx_tiles("w1")
         quantize(w1_mx, w1_b[:].rearrange("p t m j -> p (t m j)"), 0, S)
         for c0 in (0, S // 2):
             nc.vector.tensor_copy(
                 x_mx[0][:, c0 : c0 + S // 2], xw[:].indirect(offs_t[:, c0 // 16 : (c0 + S // 2) // 16])
             )
-        w2_b = keep.tile([P, PACK, P, PACK], BF16, name="w2_b", align_bytes=64)
+        w23_b = keep.tile([P, PACK, 2, P, PACK], BF16, name="w2_b", align_bytes=64)
+        w2_b, w3_b = w23_b[:, :, 0, :, :], w23_b[:, :, 1, :, :]
         deal(nc.vector.tensor_copy, w2_b, w2_raw, 0, 256)
 
         yplain = [keep.tile([P, S], F32, name=f"yplain{t}") for t in range(PACK)]
@@ -133,8 +134,11 @@ def tile_picked_joinharmrangetop2_none_p_kernel(
         hwin = [keep.tile([P, 2 * S], F32, name=f"hwin{t}") for t in range(PACK)]
         pa = [keep.tile([P, S], F32, name=f"pa{t}") for t in range(PACK)]
         recip = keep.tile([P, PACK, S], F32, name="recip")
+        num = keep.tile([P, PACK, S], F32, name="num")
         for t in range(PACK):
             nc.vector.tensor_copy(pa[t][:], ywin[t][:].indirect(n1_t[:]))
+            if t < 3:
+                nc.gpsimd.tensor_tensor(num[:, t, :], pa[t][:], ywin[t][:, :S], ALU.mult)
 
         def denominator(t):
             ysq = hwin[t][:, S:]
@@ -144,17 +148,21 @@ def tile_picked_joinharmrangetop2_none_p_kernel(
             den = turn_sum(ps_fw, [pasq[:], ysq], "fw")
             root = ring.tile([P, S], F32, name="root")
             nc.scalar.activation(root[:], den[:], ACT.Abs_reciprocal_sqrt, scale=0.5, bias=0.25)
-            back = turn_sum(ps_bk, [root[:]], "bk")
-            nc.scalar.activation(recip[:, t, :], back[:], ACT.Square)
+            if t < 3:
+                nc.scalar.activation(root[:], root[:], ACT.Square)
+                back = turn_sum(ps_bk, [root[:]], "bk")
+                nc.scalar.activation(recip[:, t, :], back[:], ACT.Copy, scale=gn_t[:, t : t + 1])
+            else:
+                back = turn_sum(ps_bk, [root[:]], "bk")
+                nc.scalar.activation(recip[:, t, :], back[:], ACT.Square)
 
-        num = keep.tile([P, PACK, S], F32, name="num")
         upper = keep.tile([P, PACK, S], F32, name="upper")
         lower = keep.tile([P, PACK, S], F32, name="lower", align_bytes=64)
         gm_half = keep.tile([P, 2, PACK], F32, name="gm_half")
         nc.scalar.activation(gm_half[:, 0, :], gm_t[:], ACT.Copy, scale=0.5)
         nc.scalar.activation(gm_half[:, 1, :], gm_t[:], ACT.Copy, scale=-0.5)
         diffs = [[keep.tile([P, S], F32, name=f"diff{t % 2}{i}") for i in range(2)] for t in range(PACK)]
-        lows = [keep.tile([P, S], F32, name=f"low{t % 2}") for t in range(PACK)]
+        lows = [keep.tile([P, S], F32, name=f"low{t}") for t in range(PACK)]
         highs = [keep.tile([P, S], F32, name=f"high{t}") for t in range(PACK)]
         yhalf = [keep.tile([P, S], F32, name=f"yhalf{t}") for t in range(PACK)]
 
@@ -171,15 +179,21 @@ def tile_picked_joinharmrangetop2_none_p_kernel(
                 num[:, t, :], pa[t][:], gn_t[:, t : t + 1], yplain[t][:], ALU.mult, ALU.mult
             )
 
-        w3_b = keep.tile([P, PACK, P, PACK], BF16, name="w3_b", align_bytes=64)
         for t in range(PACK):
             denominator(t)
             if t >= 0:
                 nc.scalar.activation(yhalf[t][:], ywin[t][:, :S], ACT.Copy, scale=gm_half[:, 0, t : t + 1])
+        for c0 in range(256, S, P):
+            deal(nc.scalar.copy, w2_b, w2_raw, c0, c0 + P)
         for t in range(PACK):
-            fetch_diff(t, 0)
+            deal(nc.scalar.copy, w3_b, w3_raw, t * P, (t + 1) * P)
+        fetch_diff(0, 0)
+        for t in range(PACK):
             fetch_diff(t, 1)
-            numerator(t)
+            if t + 1 < PACK:
+                fetch_diff(t + 1, 0)
+            if t >= 3:
+                numerator(t)
             extreme(t, highs, ALU.max)
             extreme(t, lows, ALU.min)
             if t >= 0:
@@ -193,10 +207,6 @@ def tile_picked_joinharmrangetop2_none_p_kernel(
                 back = turn_sum(ps_bk, [turned[:]], "bk")
                 nc.scalar.activation(upper[:, t, :], back[:], ACT.Copy, scale=gm_half[:, 0, t : t + 1])
             nc.scalar.activation(lower[:, t, :], lows[t][:], ACT.Copy, scale=gm_half[:, 1, t : t + 1])
-        for c0 in range(256, S, P):
-            deal(nc.scalar.copy, w2_b, w2_raw, c0, c0 + P)
-        for t in range(PACK):
-            deal(nc.scalar.copy, w3_b, w3_raw, t * P, (t + 1) * P)
 
         def combine(dst, a, b, op, c0, c1):
             nc.vector.tensor_tensor(
@@ -207,35 +217,33 @@ def tile_picked_joinharmrangetop2_none_p_kernel(
             )
 
         z_mx, z2_mx = mx_tiles("z"), mx_tiles("z2")
-        w_flat = [w[:].rearrange("p t m j -> p (t m j)") for w in (w2_b, w3_b)]
-        first_mx = [mx_tiles("w2_first", P), mx_tiles("w3_first", P)]
+        w_flat = w23_b[:].rearrange("p t w m j -> p (t w m j)")
+        first_mx = mx_tiles("w_first", 2 * P)
         z_b = keep.tile([P, S, PACK], BF16, name="z_b", align_bytes=64)
         z2_b = keep.tile([P, S, PACK], BF16, name="z2_b", align_bytes=64)
         halves = [(0, S // 2), (S // 2, S)]
         combine(z_b, num, recip, ALU.mult, 0, S)
-        for i in range(2):
-            quantize(first_mx[i], w_flat[i], 0, P)
+        quantize(first_mx, w_flat, 0, 2 * P)
         combine(z2_b, upper, lower, ALU.add, *halves[0])
         quantize(z_mx, z_b[:].rearrange("p c t -> p (c t)"), 0, S)
         combine(z2_b, upper, lower, ALU.add, *halves[1])
         for c0, c1 in halves:
             quantize(z2_mx, z2_b[:].rearrange("p c t -> p (c t)"), c0, c1)
-        late_codes = keep.tile([P, 2, S], U32, name="lower", align_bytes=64)
-        late_scales = keep.tile([P, 2, S], U8, name="late_scales", align_bytes=64)
-        late_mx = [(late_codes[:, i, :], late_scales[:, i, :]) for i in range(2)]
-        for c0, c1 in ((P, 2 * P), (2 * P, S)):
-            for i in range(2):
-                quantize(late_mx[i], w_flat[i], c0, c1)
+        late_codes = keep.tile([P, 2 * S], U32, name="lower", align_bytes=64)
+        late_scales = keep.tile([P, 2 * S], U8, name="late_scales", align_bytes=64)
+        late_mx = (late_codes, late_scales)
+        for c0, c1 in ((2 * P, S), (S, 2 * S)):
+            quantize(late_mx, w_flat, c0, c1)
 
         for (c0, c1), copy in zip(halves, (nc.scalar.copy, nc.vector.tensor_copy)):
             bank = ps_bk.tile([P, S], F32, name="bk")
-            product(bank, first_mx[1], 0, z2_mx, c0, c1, True, False)
-            product(bank, first_mx[0], 0, z_mx, c0, c1, False, True)
+            product(bank, first_mx, 1, z2_mx, c0, c1, True, False)
+            product(bank, first_mx, 0, z_mx, c0, c1, False, True)
             copy(hwin[0][:, c0:c1], bank[:, c0:c1])
         for t in range(1, PACK):
             bank = ps_mm.tile([P, S], F32, name="mm")
-            product(bank, late_mx[1], t, z2_mx, 0, S, True, False)
-            product(bank, late_mx[0], t, z_mx, 0, S, False, True)
+            product(bank, late_mx, 2 * t + 1, z2_mx, 0, S, True, False)
+            product(bank, late_mx, 2 * t, z_mx, 0, S, False, True)
             nc.scalar.copy(hwin[t][:, :S], bank[:])
 
         out_rows = out.rearrange("(p t) j -> p t j", t=PACK)

@@ -15,9 +15,13 @@ ACT = mybir.ActivationFunctionType
 
 P = 128
 PACK = 4
-T, S = 2048, 512
-BLK = S // P
-FLOPS = 3 * 2 * 512 * 512 * 512
+T = 2048
+S = 512
+HALF = S // 2
+HALVES = ((0, HALF), (HALF, S))
+LAST = PACK - 1
+GPSIMD_COLUMNS = (S, S, HALF)
+FLOPS = 3 * 2 * S * S * S
 
 
 def tile_picked_joinharmrangetop2_none_p_kernel(
@@ -29,18 +33,23 @@ def tile_picked_joinharmrangetop2_none_p_kernel(
         keep = ctx.enter_context(tc.tile_pool(name="keep", bufs=1))
         ring = ctx.enter_context(tc.tile_pool(name="ring", bufs=2))
         ps_mm = ctx.enter_context(tc.psum_pool(name="ps_mm", bufs=2))
-        ps_fw = ctx.enter_context(tc.psum_pool(name="ps_fw", bufs=4))
-        ps_bk = ctx.enter_context(tc.psum_pool(name="ps_bk", bufs=2))
+        ps_turned = ctx.enter_context(tc.psum_pool(name="ps_turned", bufs=4))
+        ps_back = ctx.enter_context(tc.psum_pool(name="ps_back", bufs=2))
 
         def load_list(src, name):
-            tl = lists.tile([P, S // 16], U16, name=name)
-            nc.sync.dma_start(tl[:], src)
-            return tl
+            offsets = lists.tile([P, S // 16], U16, name=name)
+            nc.sync.dma_start(offsets[:], src)
+            return offsets
 
         def load_weight(w, name):
             raw = keep.tile([P, PACK, S], F32, name=name)
             nc.sync.dma_start(out=raw[:], in_=w.rearrange("(p j) c -> p j c", j=PACK))
             return raw
+
+        def load_gain(gain, name):
+            by_tile = keep.tile([P, PACK], F32, name=name)
+            nc.sync.dma_start(out=by_tile[:], in_=gain.rearrange("(p t) o -> p (t o)", t=PACK))
+            return by_tile
 
         def deal(copy, grouped, raw, c0, c1):
             copy(
@@ -58,17 +67,22 @@ def tile_picked_joinharmrangetop2_none_p_kernel(
                 out=mx[0][:, c0:c1].bitcast(FP8X4), scales=mx[1][:, c0:c1], in_=grouped_flat[:, PACK * c0 : PACK * c1]
             )
 
-        def product(bank, w_mx, t, x_mx, c0, c1, start, stop):
-            cols = slice(t * P, (t + 1) * P)
+        def product(bank, w_mx, operand, moving_mx, c0, c1, start, stop):
+            cols = slice(operand * P, (operand + 1) * P)
             nc.tensor.matmul_mx(
-                out=bank[:, c0:c1], lhsT=w_mx[0][:, cols].bitcast(FP8X4), lhsT_scale=w_mx[1][:, cols],
-                rhs=x_mx[0][:, c0:c1].bitcast(FP8X4), rhs_scale=x_mx[1][:, c0:c1], start=start, stop=stop,
+                out=bank[:, c0:c1],
+                lhsT=w_mx[0][:, cols].bitcast(FP8X4),
+                lhsT_scale=w_mx[1][:, cols],
+                rhs=moving_mx[0][:, c0:c1].bitcast(FP8X4),
+                rhs_scale=moving_mx[1][:, c0:c1],
+                start=start,
+                stop=stop,
             )
 
-        def turn_sum(pool, terms, name):
-            bank = pool.tile([P, S], F32, name=name)
-            for b in range(BLK):
-                cols = slice(b * P, (b + 1) * P)
+        def turn_sum(pool, terms):
+            bank = pool.tile([P, S], F32, name="sum")
+            for c0 in range(0, S, P):
+                cols = slice(c0, c0 + P)
                 for i, term in enumerate(terms):
                     nc.tensor.matmul(
                         bank[:, cols], term[:, cols], ident[:], is_transpose=True,
@@ -76,59 +90,59 @@ def tile_picked_joinharmrangetop2_none_p_kernel(
                     )
             return bank
 
-        xs = keep.tile([P, T], U8, name="xs")
-        nc.gpsimd.memset(xs[:].bitcast(I32), 0)
-        warm = keep.tile([P, 2], F32, name="warm")
-        nc.vector.memset(warm[:, 0:1], 1.0)
+        quads = [slice(32 * quad, 32 * quad + 4) for quad in range(P // 32)]
+        xs_rows = keep.tile([P, T], U8, name="xs_rows")
+        for quad, rows in enumerate(quads):
+            nc.sync.dma_start(
+                out=xs_rows[rows, :].bitcast(I32), in_=x_scales[0, 4 * quad : 4 * quad + 4, :].bitcast(I32)
+            )
         offs_t = load_list(offs, "offs_t")
         w1_raw = load_weight(w1, "w1_raw")
-        for q in range(4):
-            nc.scalar.dma_start(
-                out=xs[32 * q : 32 * q + 4, :].bitcast(I32), in_=x_scales[0, 4 * q : 4 * q + 4, :].bitcast(I32)
-            )
-        nc.scalar.activation(warm[:, 1:2], warm[:, 0:1], ACT.Abs_reciprocal_sqrt)
+        xs = keep.tile([P, T], U8, name="xs")
+        nc.gpsimd.memset(xs[:].bitcast(I32), 0)
+        ones = keep.tile([P, S], F32, name="ones")
+        nc.vector.memset(ones[:], 1.0)
+        for rows in quads:
+            nc.vector.tensor_copy(xs[rows, :].bitcast(I32), xs_rows[rows, :].bitcast(I32))
+        ywin = [keep.tile([P, 2 * S], F32, name=f"ywin{t}") for t in range(PACK)]
+        nc.scalar.activation(ywin[0][:, S:], ones[:], ACT.Abs_reciprocal_sqrt)
         xw = keep.tile([P, T], U32, name="xw")
         nc.sync.dma_start(out=xw[:].bitcast(I32), in_=x_words[0].rearrange("p n t -> p (n t)").bitcast(I32))
         n1_t = load_list(n1, "n1_t")
-        w2_raw = load_weight(w2, "w2_raw")
-        gn_t = keep.tile([P, PACK], F32, name="gn_t")
-        nc.sync.dma_start(out=gn_t[:], in_=gn.rearrange("(p t) o -> p (t o)", t=PACK))
-        gm_t = keep.tile([P, PACK], F32, name="gm_t")
-        nc.sync.dma_start(out=gm_t[:], in_=gm.rearrange("(p t) o -> p (t o)", t=PACK))
+        gn_t = load_gain(gn, "gn_t")
+        gm_t = load_gain(gm, "gm_t")
         n2_t = load_list(n2, "n2_t")
         n3_t = load_list(n3, "n3_t")
+        w2_raw = load_weight(w2, "w2_raw")
         w3_raw = load_weight(w3, "w3_raw")
         n4_t = load_list(n4, "n4_t")
         n5_t = load_list(n5, "n5_t")
         n6_t = load_list(n6, "n6_t")
 
-        ywin = [keep.tile([P, 2 * S], F32, name=f"ywin{t}") for t in range(PACK)]
-        for t in range(PACK):
+        for t in range(1, PACK):
             nc.gpsimd.memset(ywin[t][:, S:], 0.0)
         ident = keep.tile([P, P], F32, name="ident")
         make_identity(nc, ident[:])
 
         x_mx = mx_tiles("x")
         w1_b = keep.tile([P, PACK, P, PACK], BF16, name="w1_b", align_bytes=64)
-        deal(nc.scalar.copy, w1_b, w1_raw, 0, 256)
+        deal(nc.scalar.copy, w1_b, w1_raw, 0, HALF)
         nc.vector.tensor_copy(x_mx[1][:], xs[:].indirect(offs_t[:]))
-        deal(nc.vector.tensor_copy, w1_b, w1_raw, 256, S)
+        deal(nc.vector.tensor_copy, w1_b, w1_raw, HALF, S)
         w1_mx = mx_tiles("w1")
         quantize(w1_mx, w1_b[:].rearrange("p t m j -> p (t m j)"), 0, S)
-        for c0 in (0, S // 2):
-            nc.vector.tensor_copy(
-                x_mx[0][:, c0 : c0 + S // 2], xw[:].indirect(offs_t[:, c0 // 16 : (c0 + S // 2) // 16])
-            )
-        w23_b = keep.tile([P, PACK, 2, P, PACK], BF16, name="w2_b", align_bytes=64)
+        for c0, c1 in HALVES:
+            nc.vector.tensor_copy(x_mx[0][:, c0:c1], xw[:].indirect(offs_t[:, c0 // 16 : c1 // 16]))
+        w23_b = keep.tile([P, PACK, 2, P, PACK], BF16, name="w23_b", align_bytes=64)
         w2_b, w3_b = w23_b[:, :, 0, :, :], w23_b[:, :, 1, :, :]
-        deal(nc.vector.tensor_copy, w2_b, w2_raw, 0, 256)
 
         yplain = [keep.tile([P, S], F32, name=f"yplain{t}") for t in range(PACK)]
         for t in range(PACK):
-            bank = ps_mm.tile([P, S], F32, name="mm")
-            for c0 in (0, S // 2):
-                product(bank, w1_mx, t, x_mx, c0, c0 + S // 2, True, True)
-            nc.scalar.copy(ywin[t][:, :S], bank[:])
+            for c0, c1 in HALVES if t == 0 else ((0, S),):
+                pool, tag = (ps_back, "sum") if t == 0 else (ps_mm, "mm")
+                bank = pool.tile([P, S], F32, name=tag)
+                product(bank, w1_mx, t, x_mx, c0, c1, True, True)
+                nc.scalar.copy(ywin[t][:, c0:c1], bank[:, c0:c1])
             nc.sync.dma_start(out=yplain[t][:], in_=ywin[t][:, :S])
 
         hwin = [keep.tile([P, 2 * S], F32, name=f"hwin{t}") for t in range(PACK)]
@@ -137,23 +151,24 @@ def tile_picked_joinharmrangetop2_none_p_kernel(
         num = keep.tile([P, PACK, S], F32, name="num")
         for t in range(PACK):
             nc.vector.tensor_copy(pa[t][:], ywin[t][:].indirect(n1_t[:]))
-            if t < 3:
-                nc.gpsimd.tensor_tensor(num[:, t, :], pa[t][:], ywin[t][:, :S], ALU.mult)
+            if t < LAST:
+                wide = GPSIMD_COLUMNS[t]
+                nc.gpsimd.tensor_tensor(num[:, t, :wide], pa[t][:, :wide], ywin[t][:, :wide], ALU.mult)
 
-        def denominator(t):
+        def reciprocal(t):
             ysq = hwin[t][:, S:]
             nc.scalar.activation(ysq, ywin[t][:, :S], ACT.Square)
-            pasq = ring.tile([P, S], F32, name="pasq")
+            pasq = ring.tile([P, S], F32, name="term_a")
             nc.scalar.activation(pasq[:], pa[t][:], ACT.Square)
-            den = turn_sum(ps_fw, [pasq[:], ysq], "fw")
-            root = ring.tile([P, S], F32, name="root")
-            nc.scalar.activation(root[:], den[:], ACT.Abs_reciprocal_sqrt, scale=0.5, bias=0.25)
-            if t < 3:
+            squares = turn_sum(ps_turned, [pasq[:], ysq])
+            root = ring.tile([P, S], F32, name="term_b")
+            nc.scalar.activation(root[:], squares[:], ACT.Abs_reciprocal_sqrt, scale=0.5, bias=0.25)
+            if t < LAST:
                 nc.scalar.activation(root[:], root[:], ACT.Square)
-                back = turn_sum(ps_bk, [root[:]], "bk")
+                back = turn_sum(ps_back, [root[:]])
                 nc.scalar.activation(recip[:, t, :], back[:], ACT.Copy, scale=gn_t[:, t : t + 1])
             else:
-                back = turn_sum(ps_bk, [root[:]], "bk")
+                back = turn_sum(ps_back, [root[:]])
                 nc.scalar.activation(recip[:, t, :], back[:], ACT.Square)
 
         upper = keep.tile([P, PACK, S], F32, name="upper")
@@ -174,38 +189,28 @@ def tile_picked_joinharmrangetop2_none_p_kernel(
         def extreme(t, dst, op):
             nc.vector.scalar_tensor_tensor(dst[t][:], diffs[t][0][:], 0.0, diffs[t][1][:], op, op)
 
-        def numerator(t):
-            nc.vector.scalar_tensor_tensor(
-                num[:, t, :], pa[t][:], gn_t[:, t : t + 1], yplain[t][:], ALU.mult, ALU.mult
-            )
-
         for t in range(PACK):
-            denominator(t)
-            if t >= 0:
-                nc.scalar.activation(yhalf[t][:], ywin[t][:, :S], ACT.Copy, scale=gm_half[:, 0, t : t + 1])
-        for c0 in range(256, S, P):
-            deal(nc.scalar.copy, w2_b, w2_raw, c0, c0 + P)
-        for t in range(PACK):
-            deal(nc.scalar.copy, w3_b, w3_raw, t * P, (t + 1) * P)
+            reciprocal(t)
+            nc.scalar.activation(yhalf[t][:], ywin[t][:, :S], ACT.Copy, scale=gm_half[:, 0, t : t + 1])
+        for grouped, raw in ((w2_b, w2_raw), (w3_b, w3_raw)):
+            for c0, c1 in HALVES:
+                deal(nc.scalar.copy, grouped, raw, c0, c1)
         fetch_diff(0, 0)
         for t in range(PACK):
             fetch_diff(t, 1)
-            if t + 1 < PACK:
+            if t < LAST:
                 fetch_diff(t + 1, 0)
-            if t >= 3:
-                numerator(t)
+            else:
+                nc.vector.scalar_tensor_tensor(
+                    num[:, t, :], pa[t][:], gn_t[:, t : t + 1], yplain[t][:], ALU.mult, ALU.mult
+                )
+                left, wide = LAST - 1, GPSIMD_COLUMNS[LAST - 1]
+                nc.vector.tensor_tensor(num[:, left, wide:], pa[left][:, wide:], yplain[left][:, wide:], ALU.mult)
             extreme(t, highs, ALU.max)
             extreme(t, lows, ALU.min)
-            if t >= 0:
-                nc.vector.scalar_tensor_tensor(
-                    upper[:, t, :], highs[t][:], gm_t[:, t : t + 1], yhalf[t][:], ALU.mult, ALU.add
-                )
-            else:
-                total = turn_sum(ps_fw, [highs[t][:], highs[t][:], yplain[t][:]], "fw")
-                turned = ring.tile([P, S], F32, name="half")
-                nc.scalar.copy(turned[:], total[:])
-                back = turn_sum(ps_bk, [turned[:]], "bk")
-                nc.scalar.activation(upper[:, t, :], back[:], ACT.Copy, scale=gm_half[:, 0, t : t + 1])
+            nc.vector.scalar_tensor_tensor(
+                upper[:, t, :], highs[t][:], gm_t[:, t : t + 1], yhalf[t][:], ALU.mult, ALU.add
+            )
             nc.scalar.activation(lower[:, t, :], lows[t][:], ACT.Copy, scale=gm_half[:, 1, t : t + 1])
 
         def combine(dst, a, b, op, c0, c1):
@@ -217,110 +222,83 @@ def tile_picked_joinharmrangetop2_none_p_kernel(
             )
 
         z_mx, z2_mx = mx_tiles("z"), mx_tiles("z2")
-        w_flat = w23_b[:].rearrange("p t w m j -> p (t w m j)")
-        first_mx = mx_tiles("w_first", 2 * P)
+        w23_flat = w23_b[:].rearrange("p t w m j -> p (t w m j)")
+        first_mx = mx_tiles("w23_first", 2 * P)
         z_b = keep.tile([P, S, PACK], BF16, name="z_b", align_bytes=64)
         z2_b = keep.tile([P, S, PACK], BF16, name="z2_b", align_bytes=64)
-        halves = [(0, S // 2), (S // 2, S)]
         combine(z_b, num, recip, ALU.mult, 0, S)
-        quantize(first_mx, w_flat, 0, 2 * P)
-        combine(z2_b, upper, lower, ALU.add, *halves[0])
+        quantize(first_mx, w23_flat, 0, 2 * P)
+        combine(z2_b, upper, lower, ALU.add, *HALVES[0])
         quantize(z_mx, z_b[:].rearrange("p c t -> p (c t)"), 0, S)
-        combine(z2_b, upper, lower, ALU.add, *halves[1])
-        for c0, c1 in halves:
+        combine(z2_b, upper, lower, ALU.add, *HALVES[1])
+        for c0, c1 in HALVES:
             quantize(z2_mx, z2_b[:].rearrange("p c t -> p (c t)"), c0, c1)
-        late_codes = keep.tile([P, 2 * S], U32, name="lower", align_bytes=64)
-        late_scales = keep.tile([P, 2 * S], U8, name="late_scales", align_bytes=64)
-        late_mx = (late_codes, late_scales)
+        later_codes = keep.tile([P, 2 * S], U32, name="lower", align_bytes=64)
+        later_scales = keep.tile([P, 2 * S], U8, name="later_scales", align_bytes=64)
+        later_mx = (later_codes, later_scales)
         for c0, c1 in ((2 * P, S), (S, 2 * S)):
-            quantize(late_mx, w_flat, c0, c1)
+            quantize(later_mx, w23_flat, c0, c1)
 
-        for (c0, c1), copy in zip(halves, (nc.scalar.copy, nc.vector.tensor_copy)):
-            bank = ps_bk.tile([P, S], F32, name="bk")
-            product(bank, first_mx, 1, z2_mx, c0, c1, True, False)
-            product(bank, first_mx, 0, z_mx, c0, c1, False, True)
+        for (c0, c1), copy in zip(HALVES, (nc.scalar.copy, nc.vector.tensor_copy)):
+            bank = ps_back.tile([P, S], F32, name="sum")
+            product(bank, first_mx, 0, z_mx, c0, c1, True, False)
+            product(bank, first_mx, 1, z2_mx, c0, c1, False, True)
             copy(hwin[0][:, c0:c1], bank[:, c0:c1])
         for t in range(1, PACK):
             bank = ps_mm.tile([P, S], F32, name="mm")
-            product(bank, late_mx, 2 * t + 1, z2_mx, 0, S, True, False)
-            product(bank, late_mx, 2 * t, z_mx, 0, S, False, True)
+            product(bank, later_mx, 2 * t + 1, z2_mx, 0, S, True, False)
+            product(bank, later_mx, 2 * t, z_mx, 0, S, False, True)
             nc.scalar.copy(hwin[t][:, :S], bank[:])
 
         out_rows = out.rearrange("(p t) j -> p t j", t=PACK)
 
-        pieces = [(0, 0, S), (1, 0, S), (2, 0, S), (3, 0, S)]
-        vals = [dict() for u in pieces]
+        def row_tiles(name):
+            return [keep.tile([P, S], F32, name=f"{name}{t}") for t in range(PACK)]
 
-        def fresh(u, name):
-            tl = keep.tile([P, pieces[u][2] - pieces[u][1]], F32, name=f"{name}{u}")
-            vals[u][name] = tl
-            return tl[:]
+        b1, x, gap, hi, g = row_tiles("b1"), row_tiles("x"), row_tiles("gap"), row_tiles("hi"), row_tiles("g")
+        q, rise, result = b1, x, gap
 
-        def looked_up(u, lst):
-            t, c0, c1 = pieces[u]
-            return hwin[t][:].indirect(lst[:, c0 // 16 : c1 // 16])
+        def fetch_b1(t):
+            nc.vector.tensor_copy(b1[t][:], hwin[t][:].indirect(n4_t[:]))
 
-        def step_b(u):
-            nc.vector.tensor_copy(fresh(u, "b1"), looked_up(u, n4_t))
+        def fetch_x(t):
+            nc.vector.tensor_tensor(x[t][:], hwin[t][:].indirect(n5_t[:]), b1[t][:], ALU.subtract)
+            nc.scalar.activation(gap[t][:], x[t][:], ACT.Abs, scale=0.5)
 
-        def step_x(u):
-            nc.vector.tensor_tensor(fresh(u, "x"), looked_up(u, n5_t), vals[u]["b1"][:], ALU.subtract)
-            nc.scalar.activation(fresh(u, "gap"), vals[u]["x"][:], ACT.Abs, scale=0.5)
+        def make_hi(t):
+            nc.vector.scalar_tensor_tensor(hi[t][:], x[t][:], 0.0, b1[t][:], ALU.max, ALU.add)
 
-        def step_h(u):
-            nc.vector.scalar_tensor_tensor(fresh(u, "hi"), vals[u]["x"][:], 0.0, vals[u]["b1"][:], ALU.max, ALU.add)
+        def fetch_g(t):
+            nc.vector.tensor_tensor(g[t][:], hwin[t][:].indirect(n6_t[:]), hi[t][:], ALU.subtract)
 
-        def step_g(u):
-            nc.vector.tensor_tensor(fresh(u, "g"), looked_up(u, n6_t), vals[u]["hi"][:], ALU.subtract)
+        def make_q(t):
+            nc.vector.scalar_tensor_tensor(q[t][:], g[t][:], -0.5, gap[t][:], ALU.mult, ALU.min)
 
-        def step_q(u):
-            v = vals[u]
-            nc.vector.scalar_tensor_tensor(v["b1"][:], v["g"][:], -0.5, v["gap"][:], ALU.mult, ALU.min)
+        def finish_by_transposes(t):
+            relu_g = ring.tile([P, S], F32, name="term_a")
+            nc.scalar.activation(relu_g[:], g[t][:], ACT.Relu, scale=2.0)
+            relu_q = ring.tile([P, S], F32, name="term_b")
+            nc.scalar.activation(relu_q[:], q[t][:], ACT.Relu, scale=2.0)
+            total = turn_sum(ps_turned, [relu_q[:], relu_g[:], hi[t][:]])
+            turned = ring.tile([P, S], F32, name="turned")
+            nc.scalar.activation(turned[:], total[:], ACT.Copy, scale=0.5)
+            back = turn_sum(ps_back, [turned[:]])
+            done = ring.tile([P, S], F32, name="done")
+            nc.scalar.copy(done[:], back[:])
+            nc.sync.dma_start(out=out_rows[:, t, :], in_=done[:])
 
-        def turn_top(u):
-            v = vals[u]
-            rg = ring.tile([P, S], F32, name="pasq")
-            nc.scalar.activation(rg[:], v["g"][:], ACT.Relu, scale=2.0)
-            top = turn_sum(ps_fw, [rg[:], v["hi"][:]], "fw")
-            v["top"] = ring.tile([P, S], F32, name="half")
-            nc.scalar.activation(v["top"][:], top[:], ACT.Copy, scale=0.5)
+        def make_rise(t):
+            nc.vector.tensor_tensor(rise[t][:], q[t][:], g[t][:], ALU.max)
 
-        def turn_rest(u):
-            v = vals[u]
-            rest = turn_sum(ps_fw, [v["b1"][:]], "fw")
-            rq = ring.tile([P, S], F32, name="root")
-            nc.scalar.activation(rq[:], rest[:], ACT.Relu)
-            back = turn_sum(ps_bk, [rq[:], v["top"][:]], "bk")
-            res = ring.tile([P, S], F32, name="res")
-            nc.scalar.copy(res[:], back[:])
-            nc.sync.dma_start(out=out_rows[:, pieces[u][0], :], in_=res[:])
-
-        def turn_all(u):
-            v = vals[u]
-            rg = ring.tile([P, S], F32, name="pasq")
-            nc.scalar.activation(rg[:], v["g"][:], ACT.Relu, scale=2.0)
-            rq = ring.tile([P, S], F32, name="root")
-            nc.scalar.activation(rq[:], v["b1"][:], ACT.Relu, scale=2.0)
-            total = turn_sum(ps_fw, [rq[:], rg[:], v["hi"][:]], "fw")
-            half = ring.tile([P, S], F32, name="half")
-            nc.scalar.activation(half[:], total[:], ACT.Copy, scale=0.5)
-            back = turn_sum(ps_bk, [half[:]], "bk")
-            res = ring.tile([P, S], F32, name="res")
-            nc.scalar.copy(res[:], back[:])
-            nc.sync.dma_start(out=out_rows[:, pieces[u][0], :], in_=res[:])
-
-        def step_s(u):
-            v = vals[u]
-            nc.vector.tensor_tensor(v["x"][:], v["b1"][:], v["g"][:], ALU.max)
-
-        def step_r(u):
-            v = vals[u]
-            for c0, c1 in halves if u == PACK - 1 else [(0, S)]:
+        def finish_on_vector(t):
+            for c0, c1 in HALVES if t == LAST else ((0, S),):
                 nc.vector.scalar_tensor_tensor(
-                    v["gap"][:, c0:c1], v["hi"][:, c0:c1], 0.5, v["x"][:, c0:c1], ALU.mult, ALU.add
+                    result[t][:, c0:c1], hi[t][:, c0:c1], 0.5, rise[t][:, c0:c1], ALU.mult, ALU.add
                 )
-                nc.sync.dma_start(out=out_rows[:, u, c0:c1], in_=v["gap"][:, c0:c1])
+                nc.sync.dma_start(out=out_rows[:, t, c0:c1], in_=result[t][:, c0:c1])
 
-        steps = dict(b=step_b, x=step_x, h=step_h, g=step_g, q=step_q, s=step_s, r=step_r, t=turn_top, e=turn_rest, a=turn_all)
-        for word in "b0 b1 x0 x1 h0 h1 g0 g1 q0 q1 a0 a1 b2 b3 x2 x3 h2 h3 g2 g3 q2 q3 s2 s3 r2 r3".split():
-            steps[word[0]](int(word[1]))
+        shared_steps = (fetch_b1, fetch_x, make_hi, fetch_g, make_q)
+        for pair, last_steps in (((0, 1), (finish_by_transposes,)), ((2, 3), (make_rise, finish_on_vector))):
+            for step in shared_steps + last_steps:
+                for t in pair:
+                    step(t)

from contextlib import ExitStack

import concourse.mybir as mybir
from concourse.masks import make_identity

F32 = mybir.dt.float32
BF16 = mybir.dt.bfloat16
I32 = mybir.dt.int32
U32 = mybir.dt.uint32
U16 = mybir.dt.uint16
U8 = mybir.dt.uint8
FP8X4 = mybir.dt.float8_e4m3fn_x4
ALU = mybir.AluOpType
ACT = mybir.ActivationFunctionType

P = 128
PACK = 4
T = 2048
S = 512
HALF = S // 2
HALVES = ((0, HALF), (HALF, S))
LAST = PACK - 1
GPSIMD_COLUMNS = (S, S, HALF)
FLOPS = 3 * 2 * S * S * S


def tile_picked_joinharmrangetop2_none_p_kernel(
    tc, x_words, x_scales, w1, gn, gm, w2, w3, offs, n1, n2, n3, n4, n5, n6, out
):
    nc = tc.nc
    with ExitStack() as ctx:
        lists = ctx.enter_context(tc.tile_pool(name="lists", bufs=1))
        keep = ctx.enter_context(tc.tile_pool(name="keep", bufs=1))
        ring = ctx.enter_context(tc.tile_pool(name="ring", bufs=2))
        ps_mm = ctx.enter_context(tc.psum_pool(name="ps_mm", bufs=2))
        ps_turned = ctx.enter_context(tc.psum_pool(name="ps_turned", bufs=4))
        ps_back = ctx.enter_context(tc.psum_pool(name="ps_back", bufs=2))

        def load_list(src, name):
            offsets = lists.tile([P, S // 16], U16, name=name)
            nc.sync.dma_start(offsets[:], src)
            return offsets

        def load_weight(w, name):
            raw = keep.tile([P, PACK, S], F32, name=name)
            nc.sync.dma_start(out=raw[:], in_=w.rearrange("(p j) c -> p j c", j=PACK))
            return raw

        def load_gain(gain, name):
            by_tile = keep.tile([P, PACK], F32, name=name)
            nc.sync.dma_start(out=by_tile[:], in_=gain.rearrange("(p t) o -> p (t o)", t=PACK))
            return by_tile

        def deal(copy, grouped, raw, c0, c1):
            copy(
                out=grouped[:, :, c0 // PACK : c1 // PACK, :].rearrange("p t m j -> p m t j"),
                in_=raw[:, :, c0:c1].rearrange("p j (m t) -> p m t j", t=PACK),
            )

        def mx_tiles(name, width=S):
            codes = keep.tile([P, width], U32, name=name + "_codes", align_bytes=64)
            scales = keep.tile([P, width], U8, name=name + "_scales", align_bytes=64)
            return codes, scales

        def quantize(mx, grouped_flat, c0, c1):
            nc.vector.quantize_mx(
                out=mx[0][:, c0:c1].bitcast(FP8X4), scales=mx[1][:, c0:c1], in_=grouped_flat[:, PACK * c0 : PACK * c1]
            )

        def product(bank, w_mx, operand, moving_mx, c0, c1, start, stop):
            cols = slice(operand * P, (operand + 1) * P)
            nc.tensor.matmul_mx(
                out=bank[:, c0:c1],
                lhsT=w_mx[0][:, cols].bitcast(FP8X4),
                lhsT_scale=w_mx[1][:, cols],
                rhs=moving_mx[0][:, c0:c1].bitcast(FP8X4),
                rhs_scale=moving_mx[1][:, c0:c1],
                start=start,
                stop=stop,
            )

        def turn_sum(pool, terms):
            bank = pool.tile([P, S], F32, name="sum")
            for c0 in range(0, S, P):
                cols = slice(c0, c0 + P)
                for i, term in enumerate(terms):
                    nc.tensor.matmul(
                        bank[:, cols], term[:, cols], ident[:], is_transpose=True,
                        start=(i == 0), stop=(i == len(terms) - 1),
                    )
            return bank

        quads = [slice(32 * quad, 32 * quad + 4) for quad in range(P // 32)]
        xs_rows = keep.tile([P, T], U8, name="xs_rows")
        for quad, rows in enumerate(quads):
            nc.sync.dma_start(
                out=xs_rows[rows, :].bitcast(I32), in_=x_scales[0, 4 * quad : 4 * quad + 4, :].bitcast(I32)
            )
        offs_t = load_list(offs, "offs_t")
        w1_raw = load_weight(w1, "w1_raw")
        xs = keep.tile([P, T], U8, name="xs")
        nc.gpsimd.memset(xs[:].bitcast(I32), 0)
        ones = keep.tile([P, S], F32, name="ones")
        nc.vector.memset(ones[:], 1.0)
        for rows in quads:
            nc.vector.tensor_copy(xs[rows, :].bitcast(I32), xs_rows[rows, :].bitcast(I32))
        ywin = [keep.tile([P, 2 * S], F32, name=f"ywin{t}") for t in range(PACK)]
        nc.scalar.activation(ywin[0][:, S:], ones[:], ACT.Abs_reciprocal_sqrt)
        xw = keep.tile([P, T], U32, name="xw")
        nc.sync.dma_start(out=xw[:].bitcast(I32), in_=x_words[0].rearrange("p n t -> p (n t)").bitcast(I32))
        n1_t = load_list(n1, "n1_t")
        gn_t = load_gain(gn, "gn_t")
        gm_t = load_gain(gm, "gm_t")
        n2_t = load_list(n2, "n2_t")
        n3_t = load_list(n3, "n3_t")
        w2_raw = load_weight(w2, "w2_raw")
        w3_raw = load_weight(w3, "w3_raw")
        n4_t = load_list(n4, "n4_t")
        n5_t = load_list(n5, "n5_t")
        n6_t = load_list(n6, "n6_t")

        for t in range(1, PACK):
            nc.gpsimd.memset(ywin[t][:, S:], 0.0)
        ident = keep.tile([P, P], F32, name="ident")
        make_identity(nc, ident[:])

        x_mx = mx_tiles("x")
        w1_b = keep.tile([P, PACK, P, PACK], BF16, name="w1_b", align_bytes=64)
        deal(nc.scalar.copy, w1_b, w1_raw, 0, HALF)
        nc.vector.tensor_copy(x_mx[1][:], xs[:].indirect(offs_t[:]))
        deal(nc.vector.tensor_copy, w1_b, w1_raw, HALF, S)
        w1_mx = mx_tiles("w1")
        quantize(w1_mx, w1_b[:].rearrange("p t m j -> p (t m j)"), 0, S)
        for c0, c1 in HALVES:
            nc.vector.tensor_copy(x_mx[0][:, c0:c1], xw[:].indirect(offs_t[:, c0 // 16 : c1 // 16]))
        w23_b = keep.tile([P, PACK, 2, P, PACK], BF16, name="w23_b", align_bytes=64)
        w2_b, w3_b = w23_b[:, :, 0, :, :], w23_b[:, :, 1, :, :]

        yplain = [keep.tile([P, S], F32, name=f"yplain{t}") for t in range(PACK)]
        for t in range(PACK):
            for c0, c1 in HALVES if t == 0 else ((0, S),):
                pool, tag = (ps_back, "sum") if t == 0 else (ps_mm, "mm")
                bank = pool.tile([P, S], F32, name=tag)
                product(bank, w1_mx, t, x_mx, c0, c1, True, True)
                nc.scalar.copy(ywin[t][:, c0:c1], bank[:, c0:c1])
            nc.sync.dma_start(out=yplain[t][:], in_=ywin[t][:, :S])

        hwin = [keep.tile([P, 2 * S], F32, name=f"hwin{t}") for t in range(PACK)]
        pa = [keep.tile([P, S], F32, name=f"pa{t}") for t in range(PACK)]
        recip = keep.tile([P, PACK, S], F32, name="recip")
        num = keep.tile([P, PACK, S], F32, name="num")
        for t in range(PACK):
            nc.vector.tensor_copy(pa[t][:], ywin[t][:].indirect(n1_t[:]))
            if t < LAST:
                wide = GPSIMD_COLUMNS[t]
                nc.gpsimd.tensor_tensor(num[:, t, :wide], pa[t][:, :wide], ywin[t][:, :wide], ALU.mult)

        def reciprocal(t):
            ysq = hwin[t][:, S:]
            nc.scalar.activation(ysq, ywin[t][:, :S], ACT.Square)
            pasq = ring.tile([P, S], F32, name="term_a")
            nc.scalar.activation(pasq[:], pa[t][:], ACT.Square)
            squares = turn_sum(ps_turned, [pasq[:], ysq])
            root = ring.tile([P, S], F32, name="term_b")
            nc.scalar.activation(root[:], squares[:], ACT.Abs_reciprocal_sqrt, scale=0.5, bias=0.25)
            if t < LAST:
                nc.scalar.activation(root[:], root[:], ACT.Square)
                back = turn_sum(ps_back, [root[:]])
                nc.scalar.activation(recip[:, t, :], back[:], ACT.Copy, scale=gn_t[:, t : t + 1])
            else:
                back = turn_sum(ps_back, [root[:]])
                nc.scalar.activation(recip[:, t, :], back[:], ACT.Square)

        upper = keep.tile([P, PACK, S], F32, name="upper")
        lower = keep.tile([P, PACK, S], F32, name="lower", align_bytes=64)
        gm_half = keep.tile([P, 2, PACK], F32, name="gm_half")
        nc.scalar.activation(gm_half[:, 0, :], gm_t[:], ACT.Copy, scale=0.5)
        nc.scalar.activation(gm_half[:, 1, :], gm_t[:], ACT.Copy, scale=-0.5)
        diffs = [[keep.tile([P, S], F32, name=f"diff{t % 2}{i}") for i in range(2)] for t in range(PACK)]
        lows = [keep.tile([P, S], F32, name=f"low{t}") for t in range(PACK)]
        highs = [keep.tile([P, S], F32, name=f"high{t}") for t in range(PACK)]
        yhalf = [keep.tile([P, S], F32, name=f"yhalf{t}") for t in range(PACK)]

        def fetch_diff(t, i):
            nc.vector.tensor_tensor(
                diffs[t][i][:], ywin[t][:].indirect((n2_t, n3_t)[i][:]), yplain[t][:], ALU.subtract
            )

        def extreme(t, dst, op):
            nc.vector.scalar_tensor_tensor(dst[t][:], diffs[t][0][:], 0.0, diffs[t][1][:], op, op)

        for t in range(PACK):
            reciprocal(t)
            nc.scalar.activation(yhalf[t][:], ywin[t][:, :S], ACT.Copy, scale=gm_half[:, 0, t : t + 1])
        for grouped, raw in ((w2_b, w2_raw), (w3_b, w3_raw)):
            for c0, c1 in HALVES:
                deal(nc.scalar.copy, grouped, raw, c0, c1)
        fetch_diff(0, 0)
        for t in range(PACK):
            fetch_diff(t, 1)
            if t < LAST:
                fetch_diff(t + 1, 0)
            else:
                nc.vector.scalar_tensor_tensor(
                    num[:, t, :], pa[t][:], gn_t[:, t : t + 1], yplain[t][:], ALU.mult, ALU.mult
                )
                left, wide = LAST - 1, GPSIMD_COLUMNS[LAST - 1]
                nc.vector.tensor_tensor(num[:, left, wide:], pa[left][:, wide:], yplain[left][:, wide:], ALU.mult)
            extreme(t, highs, ALU.max)
            extreme(t, lows, ALU.min)
            nc.vector.scalar_tensor_tensor(
                upper[:, t, :], highs[t][:], gm_t[:, t : t + 1], yhalf[t][:], ALU.mult, ALU.add
            )
            nc.scalar.activation(lower[:, t, :], lows[t][:], ACT.Copy, scale=gm_half[:, 1, t : t + 1])

        def combine(dst, a, b, op, c0, c1):
            nc.vector.tensor_tensor(
                dst[:, c0:c1, :].rearrange("p (c i) t -> p c t i", i=2),
                a[:, :, c0:c1].rearrange("p t (c i) -> p c t i", i=2),
                b[:, :, c0:c1].rearrange("p t (c i) -> p c t i", i=2),
                op,
            )

        z_mx, z2_mx = mx_tiles("z"), mx_tiles("z2")
        w23_flat = w23_b[:].rearrange("p t w m j -> p (t w m j)")
        first_mx = mx_tiles("w23_first", 2 * P)
        z_b = keep.tile([P, S, PACK], BF16, name="z_b", align_bytes=64)
        z2_b = keep.tile([P, S, PACK], BF16, name="z2_b", align_bytes=64)
        combine(z_b, num, recip, ALU.mult, 0, S)
        quantize(first_mx, w23_flat, 0, 2 * P)
        combine(z2_b, upper, lower, ALU.add, *HALVES[0])
        quantize(z_mx, z_b[:].rearrange("p c t -> p (c t)"), 0, S)
        combine(z2_b, upper, lower, ALU.add, *HALVES[1])
        for c0, c1 in HALVES:
            quantize(z2_mx, z2_b[:].rearrange("p c t -> p (c t)"), c0, c1)
        later_codes = keep.tile([P, 2 * S], U32, name="lower", align_bytes=64)
        later_scales = keep.tile([P, 2 * S], U8, name="later_scales", align_bytes=64)
        later_mx = (later_codes, later_scales)
        for c0, c1 in ((2 * P, S), (S, 2 * S)):
            quantize(later_mx, w23_flat, c0, c1)

        for (c0, c1), copy in zip(HALVES, (nc.scalar.copy, nc.vector.tensor_copy)):
            bank = ps_back.tile([P, S], F32, name="sum")
            product(bank, first_mx, 0, z_mx, c0, c1, True, False)
            product(bank, first_mx, 1, z2_mx, c0, c1, False, True)
            copy(hwin[0][:, c0:c1], bank[:, c0:c1])
        for t in range(1, PACK):
            bank = ps_mm.tile([P, S], F32, name="mm")
            product(bank, later_mx, 2 * t + 1, z2_mx, 0, S, True, False)
            product(bank, later_mx, 2 * t, z_mx, 0, S, False, True)
            nc.scalar.copy(hwin[t][:, :S], bank[:])

        out_rows = out.rearrange("(p t) j -> p t j", t=PACK)

        def row_tiles(name):
            return [keep.tile([P, S], F32, name=f"{name}{t}") for t in range(PACK)]

        b1, x, gap, hi, g = row_tiles("b1"), row_tiles("x"), row_tiles("gap"), row_tiles("hi"), row_tiles("g")
        q, rise, result = b1, x, gap

        def fetch_b1(t):
            nc.vector.tensor_copy(b1[t][:], hwin[t][:].indirect(n4_t[:]))

        def fetch_x(t):
            nc.vector.tensor_tensor(x[t][:], hwin[t][:].indirect(n5_t[:]), b1[t][:], ALU.subtract)
            nc.scalar.activation(gap[t][:], x[t][:], ACT.Abs, scale=0.5)

        def make_hi(t):
            nc.vector.scalar_tensor_tensor(hi[t][:], x[t][:], 0.0, b1[t][:], ALU.max, ALU.add)

        def fetch_g(t):
            nc.vector.tensor_tensor(g[t][:], hwin[t][:].indirect(n6_t[:]), hi[t][:], ALU.subtract)

        def make_q(t):
            nc.vector.scalar_tensor_tensor(q[t][:], g[t][:], -0.5, gap[t][:], ALU.mult, ALU.min)

        def finish_by_transposes(t):
            relu_g = ring.tile([P, S], F32, name="term_a")
            nc.scalar.activation(relu_g[:], g[t][:], ACT.Relu, scale=2.0)
            relu_q = ring.tile([P, S], F32, name="term_b")
            nc.scalar.activation(relu_q[:], q[t][:], ACT.Relu, scale=2.0)
            total = turn_sum(ps_turned, [relu_q[:], relu_g[:], hi[t][:]])
            turned = ring.tile([P, S], F32, name="turned")
            nc.scalar.activation(turned[:], total[:], ACT.Copy, scale=0.5)
            back = turn_sum(ps_back, [turned[:]])
            done = ring.tile([P, S], F32, name="done")
            nc.scalar.copy(done[:], back[:])
            nc.sync.dma_start(out=out_rows[:, t, :], in_=done[:])

        def make_rise(t):
            nc.vector.tensor_tensor(rise[t][:], q[t][:], g[t][:], ALU.max)

        def finish_on_vector(t):
            for c0, c1 in HALVES if t == LAST else ((0, S),):
                nc.vector.scalar_tensor_tensor(
                    result[t][:, c0:c1], hi[t][:, c0:c1], 0.5, rise[t][:, c0:c1], ALU.mult, ALU.add
                )
                nc.sync.dma_start(out=out_rows[:, t, c0:c1], in_=result[t][:, c0:c1])

        shared_steps = (fetch_b1, fetch_x, make_hi, fetch_g, make_q)
        for pair, last_steps in (((0, 1), (finish_by_transposes,)), ((2, 3), (make_rise, finish_on_vector))):
            for step in shared_steps + last_steps:
                for t in pair:
                    step(t)
